import numpy as np, ml_dtypes
CORES = [113,118,241,246]
N = 4
BF = ml_dtypes.bfloat16
def gentries(a):
    return np.ascontiguousarray(a.reshape(8, 16, -1).transpose(0, 2, 1)).reshape(8, -1)
def gtable(e):
    e = np.asarray(e); return np.ascontiguousarray(e.reshape(8, -1, 16).transpose(0, 2, 1)).reshape(128, -1).astype(np.int32)
K, C, NS, RO = 256, 2, 384, 6
V, W = C * K, N * C * K
def parts(rng):
    lev = rng.integers(0, 160, (N, 8, 1, W)); b = lev + ((256 - lev) * rng.random((N, 8, 16, W))).astype(np.int64)
    L = rng.integers(0, W, (N, 8, 16, NS)); S = rng.integers(0, W, (N, 8, 16, V))
    P = np.argsort(rng.random((N, 8, C, NS)), axis=-1)[..., :K].reshape(N, 8, V); Q = rng.integers(0, NS, (N, 8, V))
    return np.minimum(b, 255), L, S, P, Q, rng.integers(400, 2000, (N, 8, 16, 1)), rng.integers(1600, 2900, (N, 8, 1))
def pack(b, L, S, P, Q, th, mg):
    return {"base": np.ascontiguousarray(b.reshape(N, 128, W)).astype(np.float32).astype(BF), "favor": np.ascontiguousarray(L.reshape(N, 128, NS)).astype(np.int32),
            "src": np.ascontiguousarray(S.reshape(N, 128, V)).astype(np.int32), "grant": np.stack([gtable(a) for a in P]), "part": np.stack([gtable(a) for a in Q]),
            "th": np.ascontiguousarray(th.reshape(N, 128, 1)).astype(np.int32), "mg": mg.astype(np.int32)}
def setup_inputs(rng):
    return pack(*parts(rng))
def setup_inputs_spread(rng):
    b, L, S, P, Q, th, mg = parts(rng)
    b = np.minimum((256 * rng.random((N, 8, 16, W)) * np.exp2(-rng.integers(0, 8, (N, 8, 1, W)).astype(np.float64))).astype(np.int64), 255)
    L = np.minimum((W * rng.random(L.shape) ** 3).astype(np.int64), W - 1); S = np.minimum((W * rng.random(S.shape) ** 2).astype(np.int64), W - 1)
    Q = np.minimum((NS * rng.random(Q.shape) ** 3).astype(np.int64), NS - 1)
    th = np.minimum(np.exp2(12 * rng.random(th.shape)).astype(np.int64) - 1, 4079); mg = np.minimum(np.exp2(12 * rng.random(mg.shape)).astype(np.int64) - 1, 4079)
    return pack(b, L, S, P, Q, th, mg)
def setup_inputs_ends(rng):
    b, L, S, P, Q, th, mg = parts(rng)
    def tip(x, lo, hi, share):
        m = rng.random(x.shape); return np.where(m < 0.5 * share, lo, np.where(m < share, hi, x))
    sort_ = rng.integers(0, 5, (N, 8, 1, W)); el = 255 * rng.integers(0, 2, b.shape)
    b = np.where(sort_ == 0, 0, np.where(sort_ == 1, 255, np.where(sort_ < 4, el, tip(b, 0, 255, 0.5))))
    L = tip(L, 0, W - 1, 0.7); S = tip(S, 0, W - 1, 0.7); Q = tip(Q, 0, NS - 1, 0.8)
    ix = np.concatenate([np.arange(K // 2), np.arange(NS - K // 2, NS)]); P = rng.permuted(np.tile(ix, (N, 8, C, 1)), axis=-1).reshape(N, 8, V)
    th = tip(th, 0, 4079, 1.0); th[:, :, 15] = 4079; th[:, :, 0] = 0
    for r in range(N):
        last = 4079 if (N - 1 - r) % 2 == 0 else 0
        mg[r, :7, 0] = rng.permutation(np.array([0, 0, 0, 4079, 4079, 4079, 4079 - last])); mg[r, 7, 0] = last
    zero = rng.random((N, 8)) < 0.7; zero[:, 7] = True
    b[..., W - 1] = np.where(zero[:, :, None], 0, b[..., W - 1])
    hi = np.array([0, K + 1, K - 2, 2 * K - 1, V - 1, V - 2 - K]); lo = np.array([K, 1, 2 * K - 2, K - 1, V - 2, V - 1 - K])
    b[:, :, :, hi] = 255; b[:, :, :, lo] = 0; S[:, :, 15, hi] = W - 1; S[:, :, 15, lo] = 0
    np.put_along_axis(L[:, :, 15], P[:, :, hi], W - 1, 2)
    return pack(b, L, S, P, Q, th, mg)
def setup_inputs_corners(rng):
    b, L, S, P, Q, th, mg = parts(rng); e = np.arange(V); rev = (e // K ^ 1) * K + e % K
    for r in range(N):
        for g, k in enumerate(rng.permutation(8)):
            if k == 0: S[r, g] = e
            if k == 1:
                L[r, g] = rng.integers(0, W, (1, NS)); S[r, g] = rng.choice(np.array([0, V - 1, V, W - 1]), (16, V)); Q[r, g] = rng.choice(np.array([0, NS - 1]), V)
            if k == 2:
                b[r, g] = rng.integers(0, 4, (16, W)); th[r, g, :, 0] = rng.integers(0, 41, 16); mg[r, g, 0] = rng.integers(0, 21)
            if k == 3:
                Q[r, g] = P[r, g]; S[r, g] = rev; mg[r, g, 0] = rng.integers(0, 600)
                for c in range(C):
                    a = e[c * K:(c + 1) * K]; L[r, g][:, P[r, g, a]] = np.where(rng.random((16, K)) < 0.5, a, rev[a])
            if k == 4:
                L[r, g] = rng.integers(V, W, (16, NS)); S[r, g] = rng.integers(V, W, (16, V)); th[r, g] = 4079; mg[r, g] = 4079
            if k == 5: th[r, g] = 0; mg[r, g] = 0
            if k == 6:
                b[r, g] = 255 * rng.integers(0, 2, (16, W)); L[r, g, 8:] = L[r, g, :8]; th[r, g, :, 0] = 255 * rng.integers(0, 16, 16); mg[r, g, 0] = 255 * rng.integers(0, 9)
            if k == 7:
                b[r, g] = 8 * rng.integers(0, 32, (1, W)); th[r, g, :, 0] = 128 * rng.integers(1, 20, 16); mg[r, g, 0] = 128 * rng.integers(4, 14)
    return pack(b, L, S, P, Q, th, mg)
def setup_inputs_crowd(rng):
    b, L, S, P, Q, th, mg = parts(rng); z = (1 + (RO - 1) % (N - 1)) * V + ((RO - 1) % C) * K
    s = 490 + np.arange(64); low = (s // 16)[None, :] + (np.arange(16)[:, None] < (s % 16)[None, :]).astype(np.int64)
    for r in range(N):
        for g, k in enumerate(rng.permutation(8) % 4):
            if k == 3: continue
            b[r, g, :, :V] = rng.integers(200, 256, (16, V)); b[r, g, :, z:z + 64] = low; b[r, g, :, z + 64:z + K] = 0
            L[r, g] = z + K - 1 if k == 2 else rng.integers(z + 64, z + K, (16, NS))
            if k == 2: Q[r, g] = rng.integers(0, NS)
            c0 = (1, 0, C - 1)[k]; a = int(rng.integers(0, K)) + K * np.arange(c0, C)
            b[r, g][:, a] = 0; S[r, g][:, a] = z + rng.integers(0, 64, (16, C - c0))
            th[r, g, :, 0] = rng.integers(480, 521, 16); mg[r, g, 0] = rng.choice(np.array([0, 1, 3199]))
    return pack(b, L, S, P, Q, th, mg)
def check_inputs(d):
    bad = []; x = np.asarray(d["base"]).astype(np.float32)
    if not np.all((x >= 0) & (x <= 255) & (x == np.floor(x))): bad.append("range of base")
    for k, lo, hi in (("favor", 0, W - 1), ("src", 0, W - 1), ("grant", 0, NS - 1), ("part", 0, NS - 1), ("th", 0, 4079), ("mg", 0, 4079)):
        if np.min(d[k]) < lo or np.max(d[k]) > hi: bad.append("range of " + k)
    p = np.sort(np.stack([gentries(a) for a in d["grant"]]).astype(np.int64).reshape(N, 8, C, K), axis=-1)
    if np.any(p[..., 1:] == p[..., :-1]): bad.append("grantors of a class differ")
    return bad
def reference(base, favor, src, grant, part, th, mg):
    b = base.astype(np.float32).astype(np.int64).reshape(N, 8, 16, W); X = b + 0
    L = favor.astype(np.int64).reshape(N, 8, 16, NS); S = src.astype(np.int64).reshape(N, 8, 16, V)
    P = np.stack([gentries(a) for a in grant]).astype(np.int64); Q = np.stack([gentries(a) for a in part]).astype(np.int64)
    lim = th.astype(np.int64).reshape(N, 8, 16, 1); gap = mg.astype(np.int64).reshape(N, 8, 1); A = np.zeros((N, 8), np.int64); lane = np.arange(K)
    for t in range(RO):
        c = t % C; o = c * K; v = (c ^ 1) * K; e = o + lane; be = b[..., o:o + K]; old = X[..., o:o + K] + 0; s = S[..., o:o + K] + 0
        far = np.take_along_axis(X, s.reshape(N, 8, 1, 16 * K), 3).reshape(N, 8, 16, 16, K)
        dist = np.sum(np.abs(far - old[:, :, :, None, :]), axis=2)
        lapse = dist > lim + (A & 31)[:, :, None, None]
        x = np.where(lapse, be, old); s = np.where(lapse, e, s)
        pe = P[:, :, None, o:o + K]; T = np.take_along_axis(L, pe, 3)
        y = np.take_along_axis(X, T.reshape(N, 8, 1, 16 * K), 3).reshape(N, 8, 16, 16, K)
        k1 = np.argmin(y, axis=3); least = np.min(y, axis=3); less = least < x
        x = np.where(less, least, x); s = np.where(less, np.take_along_axis(T, k1, 2), s)
        den = np.sum(be - x, axis=2) - np.sum(b[..., v:v + K] - X[..., v:v + K], axis=2) > gap
        k2 = np.sum(y[:, :, :, 0, :], axis=2) & 15
        new = np.take_along_axis(np.take_along_axis(L, Q[:, :, None, o:o + K], 3), k2[:, :, None, :], 2)
        put = den[:, :, None, :] & (np.arange(16)[:, None] == ((lane + t) & 15)[None, :])
        np.put_along_axis(L, np.broadcast_to(pe, T.shape), np.where(put, new, T), 3)
        x = np.where(den[:, :, None, :], be, x); s = np.where(den[:, :, None, :], e, s); A = A + np.sum(den, axis=2)
        d = 1 + t % (N - 1)
        X[..., o:o + K] = x; S[..., o:o + K] = s; X[..., d * V + o:d * V + o + K] = np.roll(x, d, axis=0)
    return {"yx": X.reshape(N, 128, W).astype(np.float32).astype(BF), "ys": S.reshape(N, 128, V).astype(np.float32), "yl": L.reshape(N, 128, NS).astype(np.float32)}

@@ -1,0 +1,616 @@
+from concourse.mybir import AluOpType, ActivationFunctionType
+
+ALU = AluOpType
+ACT = ActivationFunctionType
+K, C, NS, RO, NR = 256, 2, 384, 6, 4
+V, WN = C * K, NR * C * K
+U = 65536.0
+M16 = 1.5 * 2.0 ** 39
+M0 = 1.5 * 2.0 ** 23
+M5 = 1.5 * 2.0 ** 28
+M6 = 1.5 * 2.0 ** 29
+ZS = 2048.0
+CH = [(0, 64), (64, 128), (128, 192), (192, 256)]
+TG = [(0, 128), (128, 256)]
+OPT = {"put": "a", "h": "a", "src": "round", "dvl": 0, "one": 0}
+
+F, B, H, I32, U16 = "float32", "bfloat16", "float16", "int32", "uint16"
+SCRATCH = {
+    "ps": ("psum", [128, 4096], F),
+    "W": ("sbuf", [128, WN], F),
+    "bs": ("sbuf", [128, WN], B),
+    "bu": ("sbuf", [128, V], B),
+    "fav": ("sbuf", [128, NS], I32),
+    "sr": ("sbuf", [128, V], I32),
+    "gp": ("sbuf", [128, 64], I32),
+    "gq": ("sbuf", [128, 64], U16),
+    "tm": ("sbuf", [128, 8], I32),
+    "ci": ("sbuf", [128, 16], I32),
+    "cf": ("sbuf", [128, 64], F),
+    "L": ("sbuf", [128, NS], F),
+    "s16": ("sbuf", [128, V], U16),
+    "tu": ("sbuf", [128, K], U16),
+    "t16": ("sbuf", [128, K], H),
+    "t32": ("sbuf", [128, K], F),
+    "far": ("sbuf", [128, 4096], B),
+    "ad": ("sbuf", [128, 4096], B),
+    "ya": ("sbuf", [128, 2048], F),
+    "yb": ("sbuf", [128, 2048], F),
+    "sc": ("sbuf", [128, 2048], F),
+    "step": ("sbuf", [128, 1024], B),
+    "kb": ("sbuf", [128, V], F),
+    "ko": ("sbuf", [128, V], F),
+    "u1": ("sbuf", [128, K], F),
+    "x2": ("sbuf", [128, K], B),
+    "x2u": ("sbuf", [128, K], B),
+    "xm": ("sbuf", [128, 128], B),
+    "fb": ("sbuf", [128, K], F),
+    "k3": ("sbuf", [128, K], I32),
+    "si": ("sbuf", [128, K], I32),
+    "sf": ("sbuf", [128, V], F),
+    "x3": ("sbuf", [128, RO * K], B),
+    "land": ("sbuf", [128, RO * K], B),
+    "outb": ("sbuf", [128, RO * K], B),
+    "put": ("sbuf", [128, K], B),
+    "ee": ("sbuf", [128, K], F),
+    "i1": ("sbuf", [128, K], F),
+    "y0": ("sbuf", [128, K], B),
+    "j1": ("sbuf", [128, K], F),
+    "j2": ("sbuf", [128, K], F),
+    "eq": ("sbuf", [128, K], F),
+    "sel": ("sbuf", [128, K], H),
+    "sg": ("sbuf", [128, K], B),
+    "lane": ("sbuf", [128, K], B),
+    "gi": ("sbuf", [128, 128], B),
+    "jm": ("sbuf", [128, 272], B),
+    "nm": ("sbuf", [128, 272], B),
+    "one": ("sbuf", [128, 144], B),
+    "cst": ("sbuf", [128, K], B),
+    "mb": ("sbuf", [128, 288], B),
+    "mh": ("sbuf", [128, 288], H),
+    "wb": ("sbuf", [128, 144], B),
+    "mat": ("sbuf", [128, 12 * 128], B),
+    "math": ("sbuf", [128, 2 * 128], H),
+}
+ENGINES = ["g", "v", "a", "p", "s"]
+NDMA = 28
+SEMAPHORES = ["e_" + e for e in ENGINES] + ["d%d" % i for i in range(NDMA)] + \
+    ["arr%d" % i for i in range(RO * len(TG))] + ["sent"]
+
+ID, UI, NI, BP, BN, BH, DR, DHI, DLO, E8, MGH, MGL = range(12)
+
+
+def rank_program(g, core, T, topo):
+    rank = T.rank_of(core)
+    if rank is None:
+        return
+    ops = []
+    queue = {"g": g, "v": g.vector, "a": g.scalar, "p": g.tensor, "s": g.sync}
+    DVL = OPT["dvl"]
+
+    def R(name, a=None, b=None, step=1, parts=128):
+        n = T[name].shape[1]
+        a = 0 if a is None else a
+        b = n if b is None else b
+        ap = T[name][0:parts, a:b:step] if step > 1 else T[name][0:parts, a:b]
+        return (ap, [(name, a, b)])
+
+    def IX(win, off):
+        return (win[0].indirect(off[0]), win[1], off[1])
+
+    def PS(bank, a, b):
+        return R("ps", 512 * bank + a, 512 * bank + b)
+
+    def MAT(i, parts=128):
+        return R("mat", 128 * i, 128 * i + 128, parts=parts)
+
+    def COL(i, parts=128, n=1):
+        return R("cf", i, i + n, parts=parts)
+
+    def add(eng, fn, outs, ins, dma=False, ext=None):
+        rd, wr = [], []
+        for o in outs:
+            wr += o[1]
+            if len(o) > 2:
+                rd += o[2]
+        for o in ins:
+            if isinstance(o, tuple):
+                rd += o[1]
+                if len(o) > 2:
+                    rd += o[2]
+        ops.append({"e": eng, "fn": fn, "rd": rd, "wr": wr, "dma": dma, "ext": ext})
+
+    def ap(o):
+        return o[0] if isinstance(o, tuple) else o
+
+    def tt(out, a, b, op, ext=None):
+        add("v", lambda q: q.tensor_tensor(out[0], a[0], b[0], op), [out], [a, b], ext=ext)
+
+    def ts(out, a, s1, op0, s2=None, op1=None, ext=None):
+        if s2 is None:
+            add("v", lambda q: q.tensor_scalar(out[0], a[0], ap(s1), None, op0), [out], [a, s1], ext=ext)
+        else:
+            add("v", lambda q: q.tensor_scalar(out[0], a[0], ap(s1), ap(s2), op0, op1), [out], [a, s1, s2], ext=ext)
+
+    def cp(out, a):
+        add("v", lambda q: q.tensor_copy(out[0], a[0]), [out], [a])
+
+    def fill(out, val):
+        add("v", lambda q: q.memset(out[0], val), [out], [])
+
+    def act(out, a, func=ACT.Identity, bias=0.0, scale=1.0, acc=None, ext=None):
+        if acc is None:
+            add("a", lambda q: q.activation(out[0], a[0], func, bias=ap(bias), scale=ap(scale)), [out], [a, bias, scale], ext=ext)
+        else:
+            add("a", lambda q: q.activation(out[0], a[0], func, bias=ap(bias), scale=ap(scale), accum_out=acc[0]),
+                [out, acc], [a, bias, scale])
+
+    def mm(out, pairs, first=True, last=True):
+        for j, (l, r) in enumerate(pairs):
+            st, sp = first and j == 0, last and j == len(pairs) - 1
+            add("p", lambda q, l=l, r=r, st=st, sp=sp: q.matmul(out[0], l[0], r[0], st, sp), [out], [l, r])
+
+    def load(eng, out, src):
+        add(eng, lambda q: q.dma_start(out[0], src), [out], [], dma=True)
+
+    def store(eng, dst, src, ext=None):
+        add(eng, lambda q: q.dma_start(dst, src[0]), [], [src], dma=True, ext=ext)
+
+    def iota(out, pattern, base, cm, whole=False):
+        if whole:
+            add("g", lambda q: q.iota(out[0], pattern, base, cm), [out], [])
+        else:
+            add("g", lambda q: q.iota(out[0], pattern, base, cm, allow_small_or_imprecise_dtypes=True), [out], [])
+
+    emask = -1
+    for other in T.cores:
+        if other != core:
+            emask &= topo.mask(core, other)
+    neng = bin(emask).count("1")
+    nsent = [0]
+
+    def send(t, j):
+        a, b = TG[j]
+        if OPT["one"]:
+            if j == 0:
+                return
+            a = 0
+        dst = T.cores[(rank + 1 + t % (NR - 1)) % NR]
+        rid, pid = topo.addr(dst, core)
+        src = R("x3", t * K + a, t * K + b)
+        to = R("land", t * K + a, t * K + b)
+        sem = T.sem["arr%d" % (t * len(TG) + j)]
+        add("g", lambda q: q.remote_dma(to[0], src[0], sem, T.sem.sent, pid, rid, emask), [], [src], dma="remote")
+        nsent[0] += neng
+
+    def arrived(t, j=None):
+        return [(T.sem["arr%d" % (t * len(TG) + i)], neng) for i in range(OPT["one"], len(TG)) if j in (None, i)]
+
+    PCOL, RCOL, A16, C15, TF, HI, LO, AP_, T1, T2, CC, ACC = [4 * i for i in range(12)]
+    GCOL, GG = RCOL + 1, LO
+    fill(R("tm"), 0)
+    fill(R("one"), 1.0)
+    load("s", R("gp", 0, 32), T.grant[:])
+    load("a", R("fav"), T.favor[:])
+    load("s", R("tm", 0, 1), T.th[:])
+    load("a", R("bs", 0, 512), T.base[:, 0:512])
+    load("s", R("tm", 1, 2, parts=8), T.mg[:])
+    load("s", R("gp", 32, 64), T.part[:])
+    load("s", R("sr", 0, K), T.src[:, 0:K])
+    load("a", R("bs", 512, 1024), T.base[:, 512:1024])
+    load("s", R("bs", 1024, 1536), T.base[:, 1024:1536])
+    load("s", R("bs", 1536, 2048), T.base[:, 1536:2048])
+    load("s", R("sr", K, V), T.src[:, K:V])
+
+    iota(COL(PCOL), [[0, 1]], 0, 1)
+    iota(R("lane"), [[1, K]], 0, 0)
+    iota(R("ci", 0, 1), [[0, 1]], 0, 1, whole=True)
+    iota(R("gi"), [[1, 8], [0, 16]], 0, 0)
+    for h in range(2):
+        o, i = R("mb", 144 * h, 144 * h + 144), R("one")
+        add("g", lambda q, o=o, i=i, h=h: q.affine_select(o[0], i[0], [[16, 9], [-1000, 2], [-1, 8]], ALU.is_equal, 0.0,
+                                                          8 * h + 7 + 1000, -1), [o], [i])
+    iota(R("jm"), [[0, 17], [1, 16]], 0, 0)
+
+    fill(R("step"), 2048.0)
+    fill(R("cst"), -U * ZS)
+    L128 = R("lane", 0, 128)
+    ts(MAT(ID), L128, COL(PCOL), ALU.is_equal)
+    ts(R("ci", 4, 5), R("ci", 0, 1), 15, ALU.bitwise_and)
+    ts(R("ci", 5, 6), R("ci", 0, 1), 4, ALU.arith_shift_right)
+    fill(R("step", 0, 1024, 8), 2.0 ** 25)
+    cp(COL(RCOL, n=2), R("ci", 4, 6))
+    fill(COL(AP_), -15.5)
+    act(MAT(UI), MAT(ID), scale=U)
+    act(MAT(NI), MAT(ID), scale=-1.0)
+    act(COL(C15), COL(GCOL), scale=16.0, bias=15.0)
+    ts(R("math", 128, 256), L128, COL(PCOL), ALU.is_equal, -1.0, ALU.mult)
+    ts(MAT(E8, 8), R("gi", parts=8), COL(PCOL, 8), ALU.is_equal)
+    ts(MAT(BP), R("gi"), COL(GCOL), ALU.is_equal, ZS, ALU.mult)
+    ts(R("math", 0, 128), R("gi"), COL(GCOL), ALU.is_equal)
+    ts(R("wb"), R("lane", 0, 144), COL(C15), ALU.is_equal)
+    cp(R("mh"), R("mb"))
+    act(COL(A16), COL(RCOL), scale=1.0 / (16.0 * U * ZS))
+    act(MAT(BN), MAT(BP), scale=-1.0)
+    act(MAT(BH), MAT(BP), scale=1.0 / (16.0 * U * ZS))
+    act(MAT(DR), MAT(ID), scale=COL(A16))
+
+    def lists(c, win, bank):
+        cp(R("t16"), IX(win, R("gq", 16 * c, 16 * c + 16)))
+        for h in range(2):
+            mm(PS(bank, 128 * h, 128 * h + 128),
+               [(R("mh", 144 * h + 8 - 8 * b, 144 * h + 136 - 8 * b), R("t16", b, K, 2)) for b in range(2)])
+
+    cp(R("gq", 0, 32), R("gp", 0, 32))
+    ts(R("nm"), R("jm"), COL(RCOL), ALU.not_equal, -2.0 if OPT["put"] == "a" else 2.0 ** 42, ALU.mult)
+    at = [(0, 0), (0, K), (1, 0), (1, K), (2, 0), (3, 0), (4, 0), (6, 0)]
+
+    def block(blk):
+        mm(PS(at[blk][0], at[blk][1], at[blk][1] + K), [(MAT(ID), R("lane")), (MAT(UI), R("bs", K * blk, K * blk + K))])
+
+    block(0)
+    block(1)
+    lists(0, R("fav"), 5)
+    ts(COL(TF, n=2), R("tm", 0, 2), 0.5, ALU.add)
+    cp(R("gq", 32, 64), R("gp", 32, 64))
+    ts(COL(HI, n=2), COL(TF, n=2), M6, ALU.add, M6, ALU.subtract)
+    cp(R("tu"), PS(5, 0, K))
+    tt(COL(LO, n=2), COL(TF, n=2), COL(HI, n=2), ALU.subtract)
+    act(R("bu", 0, K), R("bs", 0, K), scale=U)
+    act(PS(7, K, V), R("bs", 0, K), scale=U, bias=-20480.0)
+    for blk in range(1, 8):
+        if blk > 1:
+            block(blk)
+        if blk == 1:
+            act(R("kb", 0, K), PS(0, 0, K), bias=-18432.0)
+            cp(R("s16", 0, K), R("sr", 0, K))
+        if blk == 3:
+            act(MAT(DHI), MAT(ID), scale=COL(HI))
+            act(MAT(DLO), MAT(ID), scale=COL(LO))
+        if blk % 2:
+            for b in (blk - 1, blk):
+                w, p = R("W", K * b, K * b + K), PS(at[b][0], at[b][1], at[b][1] + K)
+                if b in (2, 3, 5, 7):
+                    ts(w, p, float(K * b), ALU.add)
+                else:
+                    act(w, p, bias=float(K * b))
+
+    def sources(t, step):
+        o = (t % C) * K
+        if t < 0:
+            return
+        if step == 0:
+            ts(R("si"), R("k3"), 2047, ALU.bitwise_and)
+        elif t >= RO - C:
+            if step == 1:
+                cp(R("sf", o, o + K), R("si"))
+                store("s", T.ys[:, o:o + K], R("sf", o, o + K))
+        elif step == 1:
+            cp(R("s16", o, o + K), R("si"))
+        else:
+            tt(R("ko", o, o + K), PS(7, K, V), R("si"), ALU.add)
+
+    for t in range(RO):
+        c = t % C
+        o, v = c * K, (c ^ 1) * K
+        d = 1 + t % (NR - 1)
+        last = t == RO - 1
+        Ww = R("W")
+        inround = OPT["src"] == "round"
+
+        def gather(j):
+            a, b = CH[j]
+            a = max(a, DVL)
+            act(R("far", 16 * a, 16 * b), IX(Ww, R("s16", o + a, o + b)), func=ACT.Copy)
+
+        def sub(j, bank0):
+            a, b = CH[j]
+            n = b - a
+            old = R("bu", o + a, o + b) if t < C else R("x3", (t - C) * K + a, (t - C) * K + b)
+            for p in range(16):
+                at = 512 * bank0 + p * n
+                mm(R("ps", at, at + n), [(MAT(NI), old), (MAT(ID), R("far", 16 * a + p, 16 * b, 16))])
+
+        def absd(j, bank0, p0, p1):
+            a, b = CH[j]
+            n = b - a
+            act(R("ad", 16 * a + p0 * n, 16 * a + p1 * n), R("ps", 512 * bank0 + p0 * n, 512 * bank0 + p1 * n),
+                func=ACT.Abs, scale=ZS, bias=-1024.0 * ZS)
+
+        def red(j, p0, p1):
+            a, b = CH[j]
+            n = b - a
+            gj = [i for i, (ga, gb) in enumerate(TG) if ga <= a < gb][0]
+            pairs = [(MAT(DHI), R("cst", 0, n)), (MAT(DLO), R("cst", 0, n))] if p0 == 0 else []
+            pairs += [(R("wb", 15 - p, 143 - p), R("ad", 16 * a + p * n, 16 * a + (p + 1) * n)) for p in range(p0, p1)]
+            mm(PS(4 + gj, a - TG[gj][0], b - TG[gj][0]), pairs, first=p0 == 0, last=p1 == 16)
+
+        def scan(h):
+            so, d0, d1 = R("sc", 1024 * h, 1024 * h + 1024), R("step"), R("yb", 1024 * h, 1024 * h + 1024)
+            add("v", lambda q: q.tensor_tensor_scan(so[0], d0[0], d1[0], 0.0, ALU.add, ALU.min), [so], [d0, d1])
+
+        def capped(j):
+            a, b = TG[j]
+            tt(PS(7, a, b), R("sc", 8 * a + 7, 8 * b, 8), R("kb", a, b) if t == 0 else PS(6, o + a, o + b), ALU.min)
+
+        def lapsed(j):
+            a, b = TG[j]
+            tt(R("u1", a, b), PS(4 + j, 0, b - a), R("ko", o + a, o + b), ALU.max)
+
+        def favoured(j):
+            a, b = TG[j]
+            tt(PS(7, a, b), PS(7, a, b), R("u1", a, b), ALU.min)
+
+        def number(j):
+            a, b = TG[j]
+            ts(R("x2", a, b), PS(7, a, b), M16, ALU.add, M16, ALU.subtract)
+
+        def cuts(j, early):
+            a, b = TG[j]
+            n = b - a
+            if early:
+                pairs = [(MAT(BP), R("bu", o + a, o + b)), (MAT(MGH, 8), R("cst", 0, n, parts=8)), (MAT(MGL, 8), R("cst", 0, n, parts=8))]
+                if t > 0:
+                    pairs += [(MAT(BN), R("bu", v + a, v + b)), (MAT(BP), R("x3", (t - 1) * K + a, (t - 1) * K + b))]
+            else:
+                pairs = [(MAT(BN), R("x2", a, b))]
+            mm(PS(ZB[j], K, K + n), pairs, first=early, last=not early)
+
+        def direct(j, step):
+            a, b = TG[j]
+            if step == 0:
+                if last:
+                    ts(R("x2u", a, b), R("x2", a, b), 1.0 / U, ALU.mult)
+            elif step == 1:
+                tt(PS(ZB[j], 0, b - a), PS(ZB[j], K, K + b - a), R("bs" if last else "bu", o + a, o + b), ALU.min)
+            else:
+                tt(R("x3", t * K + a, t * K + b), PS(ZB[j], 0, b - a), R("x2u" if last else "x2", a, b), ALU.max)
+
+        def keys(j, step):
+            a, b = TG[j]
+            if step == 0:
+                tt(R("fb", a, b), PS(ZB[j], K, K + b - a), R("kb", o + a, o + b), ALU.min)
+            elif step == 1:
+                tt(R("k3", a, b), PS(7, a, b), R("fb", a, b), ALU.max)
+            else:
+                ts(R("x3", t * K + a, t * K + b), R("k3", a, b), M16, ALU.add, M16, ALU.subtract)
+
+        def putv(j):
+            a, b = TG[j]
+            if OPT["put"] == "v":
+                tt(R("put", a, b), PS(ZB[j], K, K + b - a), R("nm", a + t, b + t), ALU.is_gt)
+
+        def hsum(early):
+            mm(PS(HB, 0, K), [(MAT(DR), R("cst")) if early else (MAT(BH), R("y0"))], first=early, last=not early)
+
+        def chosen(step):
+            if step == 0:
+                tt(R("eq"), PS(HB, 0, K), R("j2"), ALU.is_equal)
+            else:
+                tt(R("sel"), IX(R("L"), R("gq", 32 + 16 * c, 48 + 16 * c)), R("eq"), ALU.mult)
+                mm(PS(2, K, V), [(R("math", 128, 256), R("t16")), (R("math", 0, 128), R("sel"))])
+
+        HB = 0
+        ZB = (4, 1)
+        if DVL:
+            cp(R("far", 0, 16 * DVL), IX(Ww, R("s16", o, o + DVL)))
+        gather(0)
+        for h in range(2):
+            ts(R("ya", 1024 * h, 1024 * h + 1024), IX(Ww, R("tu", 64 * h, 64 * h + 64)), -16384.0, ALU.add)
+        sub(0, 0)
+        gather(1)
+        sub(1, 2)
+        for h in range(2):
+            tt(R("yb", 1024 * h, 1024 * h + 1024), IX(Ww, R("tu", 128 + 64 * h, 192 + 64 * h)), R("ya", 1024 * h, 1024 * h + 1024), ALU.min)
+        absd(0, 0, 0, 16)
+        red(0, 0, 16)
+        gather(2)
+        sub(2, 0)
+        absd(1, 2, 0, 16)
+        red(1, 0, 16)
+        gather(3)
+        scan(0)
+        if inround:
+            sources(t - 1, 0)
+        if t == 0:
+            tt(R("ko", 0, K), PS(7, K, V), R("sr", 0, K), ALU.add)
+            ts(MAT(MGH, 8), MAT(E8, 8), COL(HI + 1, 8), ALU.mult)
+            ts(MAT(MGL, 8), MAT(E8, 8), COL(LO + 1, 8), ALU.mult)
+        lapsed(0)
+        capped(0)
+        cuts(0, True)
+        sub(3, 2)
+        favoured(0)
+        if inround:
+            sources(t - 1, 1)
+        if t == 0:
+            cp(R("L"), R("fav"))
+        number(0)
+        cuts(0, False)
+        scan(1)
+        absd(2, 0, 0, 16)
+        red(2, 0, 16)
+        cuts(1, True)
+        absd(3, 2, 0, 12)
+        red(3, 0, 12)
+        absd(3, 2, 12, 16)
+        red(3, 12, 16)
+        hsum(True)
+        a1, b1 = TG[1]
+        if last:
+            direct(0, 0)
+            direct(0, 1)
+            capped(1)
+            direct(0, 2)
+            ts(R("xm"), PS(7, a1, b1), M16, ALU.add, M16, ALU.subtract)
+        else:
+            keys(0, 0)
+            capped(1)
+            keys(0, 1)
+            ts(R("xm"), PS(7, a1, b1), M16, ALU.add, M16, ALU.subtract)
+            keys(0, 2)
+        send(t, 0)
+        putv(0)
+        if OPT["h"] == "a":
+            act(R("i1"), R("ya", 7, 2048, 8), bias=M16)
+            act(R("y0"), R("i1"), bias=-M16)
+        else:
+            ts(R("y0"), R("ya", 7, 2048, 8), M16, ALU.add, M16, ALU.subtract)
+        old = R("bu", o + a1, o + b1) if t < C else R("x3", (t - C) * K + a1, (t - C) * K + b1)
+        tt(PS(5, 128, 256), PS(5, 0, 128), old, ALU.max)
+        hsum(False)
+        tt(R("x2", a1, b1), PS(5, 128, 256), R("xm"), ALU.min)
+        cuts(1, False)
+        if inround and not last:
+            sources(t - 1, 2)
+        if t == 0:
+            cp(R("s16", K, V), R("sr", K, V))
+        if OPT["h"] == "v":
+            ts(R("j2"), PS(HB, 0, K), M0, ALU.add, M0, ALU.subtract)
+        for s in range(3):
+            direct(1, s)
+        send(t, 1)
+        if OPT["h"] == "a":
+            act(R("j1"), PS(HB, 0, K), bias=M0)
+            act(R("j2"), R("j1"), bias=-M0)
+        act(R("t32"), IX(R("L"), R("gq", 16 * c, 16 * c + 16)), func=ACT.Copy)
+        if last:
+            store("s", T.yx[:, o:o + K], R("x3", t * K, t * K + K))
+        if OPT["put"] == "v":
+            chosen(0)
+            putv(1)
+            chosen(1)
+        if last:
+            keys(0, 0)
+        keys(1, 0)
+        if OPT["put"] == "a" or not last:
+            act(R("sg"), R("fb"), func=ACT.Sign, bias=2.0 ** 20, acc=None if last else COL(ACC))
+        if OPT["put"] == "a":
+            mm(PS(3, 0, K), [(MAT(ID), R("nm", t, t + K)), (MAT(ID), R("sg"))])
+            act(R("put"), PS(3, 0, K), func=ACT.Relu)
+            chosen(0)
+            lapsed(1)
+            chosen(1)
+        else:
+            lapsed(1)
+        if last:
+            keys(0, 1)
+        favoured(1)
+        keys(1, 1)
+        if not last:
+            mm(PS(5, K, V), [(MAT(ID), R("lane")), (MAT(ID), R("x3", t * K, t * K + K))])
+            blk = 2 * d + c
+            act(PS(4, 0, K), R("lane"), bias=float(K * blk))
+            if t == 0:
+                act(PS(6, 0, V), R("W", 0, V), bias=-18432.0)
+                act(R("kb", K, V), R("W", K, V), bias=-18432.0)
+            act(R("W", o, o + K), PS(5, K, V), bias=float(o))
+        tt(R("ee"), PS(2, K, V), R("put"), ALU.mult)
+        if last or not inround:
+            sources(t, 0)
+        pd = 1 + (t - 1) % (NR - 1)
+        tt(IX(R("L"), R("gq", 16 * c, 16 * c + 16)), R("t32"), R("ee"), ALU.add)
+        if last:
+            store("s", T.yl[:], R("L"))
+            sources(t, 1)
+            act(R("outb", (t - 1) * K, t * K), R("land", (t - 1) * K, t * K), scale=1.0 / U, ext=arrived(t - 1))
+            store("a", T.yx[:, pd * V + v:pd * V + v + K], R("outb", (t - 1) * K, t * K))
+            store("a", T.yx[:, d * V + o:d * V + o + K], R("land", t * K, t * K + K), ext=arrived(t))
+            break
+        if t < RO - C:
+            act(PS(7, K, V), R("x3", t * K, t * K + K), bias=-20480.0)
+        if t == 0:
+            act(R("bu", K, V), R("bs", K, V), scale=U)
+            act(PS(3, K, V), R("bs", K, V), scale=U, bias=-20480.0)
+        a, b = TG[0]
+        if not OPT["one"]:
+            tt(R("W", K * blk + a, K * blk + b), PS(4, a, b), R("land", t * K + a, t * K + b), ALU.add, ext=arrived(t, 0))
+        lists(c ^ 1, R("L"), 0)
+        act(COL(AP_), COL(ACC), scale=0.5, bias=COL(AP_))
+        act(COL(GG), COL(ACC), scale=0.5, bias=COL(GG))
+        act(COL(T1), COL(AP_), bias=M5)
+        if t > 0:
+            act(R("outb", (t - 1) * K, t * K), R("land", (t - 1) * K, t * K), scale=1.0 / U, ext=arrived(t - 1))
+            store("s", T.yx[:, pd * V + v:pd * V + v + K], R("outb", (t - 1) * K, t * K))
+        act(COL(T2), COL(T1), bias=-M5)
+        if t == RO - C:
+            act(R("outb", (RO - 1) * K, RO * K), R("x3", t * K, t * K + K), scale=1.0 / U)
+            store("s", T.yx[:, o:o + K], R("outb", (RO - 1) * K, RO * K))
+        act(COL(CC), COL(T2), scale=-1.0, bias=COL(GG))
+        act(MAT(DLO), MAT(ID), scale=COL(CC))
+        if t == 0:
+            tt(R("ko", K, V), PS(3, K, V), R("sr", K, V), ALU.add)
+        if not inround:
+            sources(t, 1)
+            sources(t, 2)
+        cp(R("tu"), PS(0, 0, K))
+        a, b = (0, K) if OPT["one"] else TG[1]
+        tt(R("W", K * blk + a, K * blk + b), PS(4, a, b), R("land", t * K + a, t * K + b), ALU.add, ext=arrived(t, 1))
+
+    emit(ops, queue, T, nsent[0])
+
+
+def emit(ops, queue, T, nsent):
+    def meet(xs, ys):
+        return any(x[0] == y[0] and x[1] < y[2] and y[1] < x[2] for x in xs for y in ys)
+
+    def banks(x):
+        s = set()
+        for r in x["rd"] + x["wr"]:
+            if r[0] == "ps":
+                s |= set(range(r[1] // 512, (r[2] - 1) // 512 + 1))
+        return s
+
+    known = {e: {} for e in ENGINES}
+    clock, waits, signal = [], [], set()
+    bk = [banks(x) for x in ops]
+    for j, x in enumerate(ops):
+        e, need = x["e"], {}
+        for i in range(j - 1, -1, -1):
+            y = ops[i]
+            if y["e"] == "p" and ("p" in need or e == "p" or known[e].get("p", -1) >= i):
+                continue
+            if y["dma"] == "remote":
+                continue
+            key = ("dma", i) if y["dma"] else y["e"]
+            if key in need or known[e].get(key, -1) >= i or (key == "p" and e == "p"):
+                continue
+            if meet(x["rd"], y["wr"]) or meet(x["wr"], y["wr"]) or meet(x["wr"], y["rd"]) or (y["e"] != e and bk[i] & bk[j]):
+                need[key] = i
+        w = []
+        for key, i in sorted(need.items(), key=lambda kv: -kv[1]):
+            if known[e].get(key, -1) >= i:
+                continue
+            w.append(i)
+            signal.add(i)
+            for k2, i2 in clock[i].items():
+                known[e][k2] = max(known[e].get(k2, -1), i2)
+        waits.append(w)
+        ck = dict(known[e])
+        ck[("dma", j) if x["dma"] else e] = j
+        clock.append(ck)
+    count = {e: 0 for e in ENGINES}
+    mark, ndma, open_dma = {}, 0, {}
+    for j, x in enumerate(ops):
+        e, q = x["e"], queue[x["e"]]
+        for i in waits[j]:
+            sem, n = mark[i]
+            q.wait_ge(sem, n)
+            open_dma.pop(i, None)
+        for sem, n in x["ext"] or []:
+            q.wait_ge(sem, n)
+        ins = x["fn"](q)
+        if x["dma"] == "remote":
+            continue
+        if x["dma"]:
+            mark[j] = (T.sem["d%d" % ndma], 16)
+            ndma += 1
+            ins.then_inc(mark[j][0], 16)
+            open_dma[j] = e
+        elif j in signal:
+            count[e] += 1
+            mark[j] = (T.sem["e_" + e], count[e])
+            ins.then_inc(mark[j][0], 1)
+    for j, e in open_dma.items():
+        queue[e].wait_ge(*mark[j])
+    queue["g"].wait_ge(T.sem.sent, nsent)

@@ -4,80 +4,103 @@ ALU = AluOpType
 ACT = ActivationFunctionType
 K, C, NS, RO, NR = 256, 2, 384, 6, 4
 V, WN = C * K, NR * C * K
-U = 65536.0
-M16 = 1.5 * 2.0 ** 39
-M0 = 1.5 * 2.0 ** 23
+N = K // 2
+ND = 52
+HP = 64
+U = 2.0 ** 17
+TAG = 2048.0
+X0 = -128.0 * U
+WT = 10 * TAG
+M0 = 1.5 * 2.0 ** 16
 M5 = 1.5 * 2.0 ** 28
-M6 = 1.5 * 2.0 ** 29
-ZS = 2048.0
-CH = [(0, 64), (64, 128), (128, 192), (192, 256)]
-TG = [(0, 128), (128, 256)]
-OPT = {"put": "a", "h": "a", "src": "round", "dvl": 0, "one": 0}
+M7 = 1.5 * 2.0 ** 30
+XH = 1280.0
+ZS = 2.0 ** 27
+
+ORDER = """
+<cuts, <number, <<offsets, <<tally 1, far 0, <denied, low_a 0 128, <<other 2, <chosen, sub 0, <tell, <row, far_v, >>repeat,
+<reset 0, abs 0, sub 1, <own 0, <put, <reset 1, limits, high 0 128, <source, <merge, abs 1, red 0, abs_v, <own 1, red 1,
+first, <ab, entry, pick, <aged, red_v, <copies 0, <keep, <copies 1, >>>seed, <other 0, scan,
+lapsed, <edit, <sources, based, <counted, <grantors, least, <tally 0, <lay, <other 1"""
+OPENING = """
+far 0, keys 0 0 4 0, low 0 80, low_a 80 128, block 0 6 0, block 1 7 0, block 2 5 0, sub 0, constants 0, tables 0, far 1,
+keys 0 0 4 1, >seed, >repeat, >>seed, >>repeat, >>>seed, high 0 128, sub 1, abs 0, first, keys 0 0 4 2, constants 1, limits, red 0, entry, block 0 6 1, states 1 0 24,
+scan, block 1 7 1, block 3 7 0, lists 1, abs 1, red 1, layout 1, block 2 5 1, keys 1 0 5 0, block 3 7 1, origins 1 0, tile,
+keys 1 0 5 1, pick, constants 2, thresholds 1 0, lapsed, thresholds 1 1, based, keys 1 0 5 2, least, tables 1"""
+CLOSING = ["""
+far 0, <cuts, <number, <<offsets, <chosen, <<tally 1, <denied, low_a 0 128, <tell, sub 0, sub 1, <row,
+<reset 0, far_v, <reset 1, high 0 128, limits, abs 0, first, <source, red 0, scan, abs 1, red 1, abs_v, red_v, <put,
+<merge, entry, cuts, <ab, pick, lapsed, <sources, based, <keep, least""", """
+<number, <<edit, <denied, <chosen, <tell, <row, <put, <reset 0, <merge, <reset 1, <ab, <source, <keep,
+<sources, <edit"""]
 
 F, B, H, I32, U16 = "float32", "bfloat16", "float16", "int32", "uint16"
 SCRATCH = {
     "ps": ("psum", [128, 4096], F),
-    "W": ("sbuf", [128, WN], F),
+    "W": ("sbuf", [128, 2 * WN], F),
     "bs": ("sbuf", [128, WN], B),
-    "bu": ("sbuf", [128, V], B),
-    "fav": ("sbuf", [128, NS], I32),
-    "sr": ("sbuf", [128, V], I32),
-    "gp": ("sbuf", [128, 64], I32),
-    "gq": ("sbuf", [128, 64], U16),
-    "tm": ("sbuf", [128, 8], I32),
+    "bo": ("sbuf", [128, 4 * N], B),
+    "fav": ("sbuf", [128, 2 * NS], I32),
+    "sr": ("sbuf", [128, 4 * N], I32),
+    "gp": ("sbuf", [128, 128], I32),
+    "gq": ("sbuf", [128, 128], U16),
+    "gs": ("sbuf", [128, 128], U16),
+    "tm": ("sbuf", [128, 12], I32),
     "ci": ("sbuf", [128, 16], I32),
-    "cf": ("sbuf", [128, 64], F),
-    "L": ("sbuf", [128, NS], F),
-    "s16": ("sbuf", [128, V], U16),
-    "tu": ("sbuf", [128, K], U16),
-    "t16": ("sbuf", [128, K], H),
-    "t32": ("sbuf", [128, K], F),
-    "far": ("sbuf", [128, 4096], B),
-    "ad": ("sbuf", [128, 4096], B),
-    "ya": ("sbuf", [128, 2048], F),
-    "yb": ("sbuf", [128, 2048], F),
-    "sc": ("sbuf", [128, 2048], F),
-    "step": ("sbuf", [128, 1024], B),
-    "kb": ("sbuf", [128, V], F),
-    "ko": ("sbuf", [128, V], F),
-    "u1": ("sbuf", [128, K], F),
-    "x2": ("sbuf", [128, K], B),
-    "x2u": ("sbuf", [128, K], B),
-    "xm": ("sbuf", [128, 128], B),
-    "fb": ("sbuf", [128, K], F),
-    "k3": ("sbuf", [128, K], I32),
-    "si": ("sbuf", [128, K], I32),
-    "sf": ("sbuf", [128, V], F),
-    "x3": ("sbuf", [128, RO * K], B),
-    "land": ("sbuf", [128, RO * K], B),
-    "outb": ("sbuf", [128, RO * K], B),
-    "put": ("sbuf", [128, K], B),
-    "ee": ("sbuf", [128, K], F),
-    "i1": ("sbuf", [128, K], F),
-    "y0": ("sbuf", [128, K], B),
-    "j1": ("sbuf", [128, K], F),
-    "j2": ("sbuf", [128, K], F),
-    "eq": ("sbuf", [128, K], F),
-    "sel": ("sbuf", [128, K], H),
-    "sg": ("sbuf", [128, K], B),
+    "cf": ("sbuf", [128, 80], F),
+    "av": ("sbuf", [128, 16], F),
+    "L": ("sbuf", [128, 2 * NS], F),
+    "s16": ("sbuf", [128, 4 * N], U16),
+    "tu": ("sbuf", [128, 2 * N], U16),
+    "t16": ("sbuf", [128, 2 * N], H),
+    "gap": ("sbuf", [128, 2 * N], B),
+    "seed": ("sbuf", [128, 4 * N], F),
+    "rep": ("sbuf", [128, 64 * ND], F),
+    "far": ("sbuf", [128, 32 * N], B),
+    "ad": ("sbuf", [128, 32 * N], B),
+    "ya": ("sbuf", [128, 16 * N], F),
+    "yb": ("sbuf", [128, 16 * N], F),
+    "sc": ("sbuf", [128, 16 * N], F),
+    "step": ("sbuf", [128, 8 * N], B),
+    "kb": ("sbuf", [128, 4 * N], F),
+    "ko": ("sbuf", [128, 4 * N], I32),
+    "k2": ("sbuf", [128, 2 * N], I32),
+    "x2h": ("sbuf", [128, 2 * N], H),
+    "back": ("sbuf", [128, 2 * N], B),
+    "si": ("sbuf", [128, 2 * N], I32),
+    "sf": ("sbuf", [128, 4 * N], F),
+    "x3": ("sbuf", [128, 2 * RO * N], B),
+    "land": ("sbuf", [128, 2 * RO * N], B),
+    "sg": ("sbuf", [128, 4 * N], B),
+    "ab": ("sbuf", [128, V], F),
+    "h0": ("sbuf", [128, 2 * N], H),
+    "pick": ("sbuf", [128, 2 * N], F),
+    "sel": ("sbuf", [128, 2 * N], H),
+    "zero": ("sbuf", [128, K], B),
     "lane": ("sbuf", [128, K], B),
-    "gi": ("sbuf", [128, 128], B),
-    "jm": ("sbuf", [128, 272], B),
-    "nm": ("sbuf", [128, 272], B),
+    "lc": ("sbuf", [128, V], H),
+    "o2": ("sbuf", [128, 128], B),
+    "gi": ("sbuf", [128, 4 * 128], B),
+    "jm": ("sbuf", [128, 144], B),
+    "nm": ("sbuf", [128, 144], B),
     "one": ("sbuf", [128, 144], B),
-    "cst": ("sbuf", [128, K], B),
+    "cst": ("sbuf", [128, N], B),
+    "cr": ("sbuf", [128, 8 * 128], B),
     "mb": ("sbuf", [128, 288], B),
-    "mh": ("sbuf", [128, 288], H),
     "wb": ("sbuf", [128, 144], B),
-    "mat": ("sbuf", [128, 12 * 128], B),
-    "math": ("sbuf", [128, 2 * 128], H),
+    "mat": ("sbuf", [128, 22 * 128], B),
+    "math": ("sbuf", [128, 4 * 128], H),
+    "matf": ("sbuf", [128, 2 * 128], F),
 }
 ENGINES = ["g", "v", "a", "p", "s"]
-NDMA = 28
-SEMAPHORES = ["e_" + e for e in ENGINES] + ["d%d" % i for i in range(NDMA)] + \
-    ["arr%d" % i for i in range(RO * len(TG))] + ["sent"]
+NDMA = 84
+SEMAPHORES = ["e_" + e for e in ENGINES] + ["d%d" % i for i in range(NDMA)] + ["arr%d" % i for i in range(2 * RO)] + ["sent"]
 
-ID, UI, NI, BP, BN, BH, DR, DHI, DLO, E8, MGH, MGL = range(12)
+ID, UI, NI, BP, BN, BB, BKS, NKS = range(8)
+DE, UE, NE, SE, BES, MGH, MGL = range(8, 22, 2)
+DT, EV = 0, 2
+BK5, SEL = range(2)
+RR, PM0, NM0, C0, C2, CX, CH = range(7)
 
 
 def rank_program(g, core, T, topo):
@@ -86,14 +109,22 @@ def rank_program(g, core, T, topo):
         return
     ops = []
     queue = {"g": g, "v": g.vector, "a": g.scalar, "p": g.tensor, "s": g.sync}
-    DVL = OPT["dvl"]
 
-    def R(name, a=None, b=None, step=1, parts=128):
+    def R(name, a=None, b=None, step=1, parts=128, at=0):
         n = T[name].shape[1]
         a = 0 if a is None else a
         b = n if b is None else b
-        ap = T[name][0:parts, a:b:step] if step > 1 else T[name][0:parts, a:b]
-        return (ap, [(name, a, b)])
+        ap = T[name][at:at + parts, a:b:step] if step > 1 else T[name][at:at + parts, a:b]
+        return (ap, [(name, a, b, at, at + parts)])
+
+    def RH(name, h, a, b):
+        return R(name, a, b, parts=HP, at=HP * h)
+
+    def REP(m, p=None):
+        at = m // N * 16 * ND
+        if p is None:
+            return (T.rep[:, at:at + 16 * ND], [("rep%d" % i, m, m + 1, 0, 128) for i in range(16)])
+        return (T.rep[:, at + p:at + 16 * ND:16], [("rep%d" % p, m, m + 1, 0, 128)])
 
     def IX(win, off):
         return (win[0].indirect(off[0]), win[1], off[1])
@@ -101,8 +132,14 @@ def rank_program(g, core, T, topo):
     def PS(bank, a, b):
         return R("ps", 512 * bank + a, 512 * bank + b)
 
-    def MAT(i, parts=128):
-        return R("mat", 128 * i, 128 * i + 128, parts=parts)
+    def MAT(i, parts=128, name="mat"):
+        return R(name, 128 * i, 128 * i + 128, parts=parts)
+
+    def PAIR(i):
+        return R("mat", 128 * i, 128 * i + 256)
+
+    def ROW(i):
+        return MAT(i, 1, "cr")
 
     def COL(i, parts=128, n=1):
         return R("cf", i, i + n, parts=parts)
@@ -123,14 +160,14 @@ def rank_program(g, core, T, topo):
     def ap(o):
         return o[0] if isinstance(o, tuple) else o
 
-    def tt(out, a, b, op, ext=None):
-        add("v", lambda q: q.tensor_tensor(out[0], a[0], b[0], op), [out], [a, b], ext=ext)
+    def tt(out, a, b, op):
+        add("v", lambda q: q.tensor_tensor(out[0], a[0], b[0], op), [out], [a, b])
 
-    def ts(out, a, s1, op0, s2=None, op1=None, ext=None):
+    def ts(out, a, s1, op0, s2=None, op1=None):
         if s2 is None:
-            add("v", lambda q: q.tensor_scalar(out[0], a[0], ap(s1), None, op0), [out], [a, s1], ext=ext)
+            add("v", lambda q: q.tensor_scalar(out[0], a[0], ap(s1), None, op0), [out], [a, s1])
         else:
-            add("v", lambda q: q.tensor_scalar(out[0], a[0], ap(s1), ap(s2), op0, op1), [out], [a, s1, s2], ext=ext)
+            add("v", lambda q: q.tensor_scalar(out[0], a[0], ap(s1), ap(s2), op0, op1), [out], [a, s1, s2])
 
     def cp(out, a):
         add("v", lambda q: q.tensor_copy(out[0], a[0]), [out], [a])
@@ -138,17 +175,17 @@ def rank_program(g, core, T, topo):
     def fill(out, val):
         add("v", lambda q: q.memset(out[0], val), [out], [])
 
-    def act(out, a, func=ACT.Identity, bias=0.0, scale=1.0, acc=None, ext=None):
+    def act(out, a, func=ACT.Identity, bias=0.0, scale=1.0, acc=None):
         if acc is None:
-            add("a", lambda q: q.activation(out[0], a[0], func, bias=ap(bias), scale=ap(scale)), [out], [a, bias, scale], ext=ext)
+            add("a", lambda q: q.activation(out[0], a[0], func, bias=ap(bias), scale=ap(scale)), [out], [a, bias, scale])
         else:
             add("a", lambda q: q.activation(out[0], a[0], func, bias=ap(bias), scale=ap(scale), accum_out=acc[0]),
                 [out, acc], [a, bias, scale])
 
-    def mm(out, pairs, first=True, last=True):
+    def mm(out, pairs, first=True, last=True, ext=None):
         for j, (l, r) in enumerate(pairs):
             st, sp = first and j == 0, last and j == len(pairs) - 1
-            add("p", lambda q, l=l, r=r, st=st, sp=sp: q.matmul(out[0], l[0], r[0], st, sp), [out], [l, r])
+            add("p", lambda q, l=l, r=r, st=st, sp=sp: q.matmul(out[0], l[0], r[0], st, sp), [out], [l, r], ext=ext)
 
     def load(eng, out, src):
         add(eng, lambda q: q.dma_start(out[0], src), [out], [], dma=True)
@@ -163,396 +200,450 @@ def rank_program(g, core, T, topo):
             add("g", lambda q: q.iota(out[0], pattern, base, cm, allow_small_or_imprecise_dtypes=True), [out], [])
 
     emask = -1
-    for other in T.cores:
-        if other != core:
-            emask &= topo.mask(core, other)
+    for peer in T.cores:
+        if peer != core:
+            emask &= topo.mask(core, peer)
     neng = bin(emask).count("1")
-    nsent = [0]
 
-    def send(t, j):
-        a, b = TG[j]
-        if OPT["one"]:
-            if j == 0:
-                return
-            a = 0
-        dst = T.cores[(rank + 1 + t % (NR - 1)) % NR]
+    def send(n):
+        dst = T.cores[(rank + 1 + n // 2 % (NR - 1)) % NR]
         rid, pid = topo.addr(dst, core)
-        src = R("x3", t * K + a, t * K + b)
-        to = R("land", t * K + a, t * K + b)
-        sem = T.sem["arr%d" % (t * len(TG) + j)]
+        src, to, sem = R("x3", n * N, n * N + N), R("land", n * N, n * N + N), T.sem["arr%d" % n]
         add("g", lambda q: q.remote_dma(to[0], src[0], sem, T.sem.sent, pid, rid, emask), [], [src], dma="remote")
-        nsent[0] += neng
 
-    def arrived(t, j=None):
-        return [(T.sem["arr%d" % (t * len(TG) + i)], neng) for i in range(OPT["one"], len(TG)) if j in (None, i)]
+    def arrived(n):
+        return [(T.sem["arr%d" % n], neng)]
 
-    PCOL, RCOL, A16, C15, TF, HI, LO, AP_, T1, T2, CC, ACC = [4 * i for i in range(12)]
-    GCOL, GG = RCOL + 1, LO
-    fill(R("tm"), 0)
+    PCOL, RCOL, C15, TF, HI, LO, PB, S1, S2, SG, T1, EB, P4 = [4 * i for i in range(13)]
+    GCOL, G4, P64, HCOL = RCOL + 1, RCOL + 2, RCOL + 3, 60
+    ONE = R("one", 0, N, parts=1)
     fill(R("one"), 1.0)
-    load("s", R("gp", 0, 32), T.grant[:])
-    load("a", R("fav"), T.favor[:])
-    load("s", R("tm", 0, 1), T.th[:])
-    load("a", R("bs", 0, 512), T.base[:, 0:512])
-    load("s", R("tm", 1, 2, parts=8), T.mg[:])
-    load("s", R("gp", 32, 64), T.part[:])
-    load("s", R("sr", 0, K), T.src[:, 0:K])
-    load("a", R("bs", 512, 1024), T.base[:, 512:1024])
-    load("s", R("bs", 1024, 1536), T.base[:, 1024:1536])
-    load("s", R("bs", 1536, 2048), T.base[:, 1536:2048])
-    load("s", R("sr", K, V), T.src[:, K:V])
+
+    def loads(x, qa, qb):
+        rows = slice(HP * x, HP * x + HP)
+        for h in range(2):
+            load(qb, RH("gp", h, 64 * x, 64 * x + 32), T.grant[rows, :])
+        load(qa, RH("bs", x, 0, 1024), T.base[rows, 0:1024])
+        load(qa, RH("bs", x, 1024, WN), T.base[rows, 1024:WN])
+        for h in range(2):
+            load(qb, RH("fav", h, NS * x, NS * x + NS), T.favor[rows, :])
+        for h in range(2):
+            load(qb, RH("sr", h, 2 * x * N, 2 * x * N + N), T.src[rows, h * N:h * N + N])
+            load(qa, RH("bo", h, 2 * x * N, 2 * x * N + N), T.base[rows, h * N:h * N + N])
+        for h in range(2):
+            load(qb, RH("tm", h, 4 * x, 4 * x + 1), T.th[rows])
+            load(qb, RH("gp", h, 64 * x + 32, 64 * x + 64), T.part[rows, :])
+
+    def later(x):
+        rows = slice(HP * x, HP * x + HP)
+        for h in range(2):
+            load("s", RH("bo", h, (2 * x + 1) * N, (2 * x + 2) * N), T.base[rows, K + h * N:K + h * N + N])
+            load("s", RH("sr", h, (2 * x + 1) * N, (2 * x + 2) * N), T.src[rows, K + h * N:K + h * N + N])
+
+    loads(0, "a", "s")
+    load("s", R("tm", 8, 9, parts=8), T.mg[:])
+    loads(1, "s", "s")
+    later(0)
+    later(1)
 
     iota(COL(PCOL), [[0, 1]], 0, 1)
-    iota(R("lane"), [[1, K]], 0, 0)
     iota(R("ci", 0, 1), [[0, 1]], 0, 1, whole=True)
-    iota(R("gi"), [[1, 8], [0, 16]], 0, 0)
+    iota(R("gi", 256, 512), [[64, 2], [0, 2], [1, 64]], 0, 0)
+    iota(R("lane"), [[1, K]], 0, 0)
+    iota(R("gi", 0, 128), [[1, 8], [0, 16]], 0, 0)
     for h in range(2):
-        o, i = R("mb", 144 * h, 144 * h + 144), R("one")
+        o, i = R("mb", 144 * h, 144 * h + 144), R("one", 0, 144)
         add("g", lambda q, o=o, i=i, h=h: q.affine_select(o[0], i[0], [[16, 9], [-1000, 2], [-1, 8]], ALU.is_equal, 0.0,
                                                           8 * h + 7 + 1000, -1), [o], [i])
-    iota(R("jm"), [[0, 17], [1, 16]], 0, 0)
+    iota(R("jm"), [[0, 9], [1, 16]], 0, 0)
+    iota(R("gi", 128, 256), [[0, 2], [1, 4], [0, 16]], 0, 0)
+    GI, GI4, M64 = R("gi", 0, 128), R("gi", 128, 256), R("gi", 256, 512)
 
-    fill(R("step"), 2048.0)
-    fill(R("cst"), -U * ZS)
-    L128 = R("lane", 0, 128)
-    ts(MAT(ID), L128, COL(PCOL), ALU.is_equal)
+    fill(R("lc", parts=2), X0 / 4096)
+    fill(R("o2", parts=2), 4096.0)
     ts(R("ci", 4, 5), R("ci", 0, 1), 15, ALU.bitwise_and)
     ts(R("ci", 5, 6), R("ci", 0, 1), 4, ALU.arith_shift_right)
-    fill(R("step", 0, 1024, 8), 2.0 ** 25)
-    cp(COL(RCOL, n=2), R("ci", 4, 6))
-    fill(COL(AP_), -15.5)
-    act(MAT(UI), MAT(ID), scale=U)
-    act(MAT(NI), MAT(ID), scale=-1.0)
+    ts(R("ci", 6, 7), R("ci", 0, 1), 4, ALU.arith_shift_right, 3, ALU.bitwise_and)
+    ts(R("ci", 7, 8), R("ci", 0, 1), 63, ALU.bitwise_and)
+    fill(R("o2", parts=1), 1.0)
+    cp(COL(RCOL, n=4), R("ci", 4, 8))
+    cp(R("lc", 0, K, parts=1), R("lane", parts=1))
+    ts(R("lc", K, V, parts=1), R("lane", parts=1), float(K), ALU.add)
+    ts(PAIR(UE), M64, COL(PCOL), ALU.is_equal, U, ALU.mult)
+    ts(MAT(ID), R("lane", 0, 128), COL(PCOL), ALU.is_equal)
+    ts(MAT(BP), GI, COL(GCOL), ALU.is_equal, ZS, ALU.mult)
+    ts(COL(S2), COL(RCOL), 1.0, ALU.is_equal, M5, ALU.mult)
+    ts(COL(T1), COL(RCOL), 1.0, ALU.is_le)
+    act(R("cst"), R("one", 0, N), scale=-ZS)
+    act(R("av"), R("one", 0, 16), scale=0.0)
+    act(ROW(CX), ONE, scale=X0)
     act(COL(C15), COL(GCOL), scale=16.0, bias=15.0)
-    ts(R("math", 128, 256), L128, COL(PCOL), ALU.is_equal, -1.0, ALU.mult)
-    ts(MAT(E8, 8), R("gi", parts=8), COL(PCOL, 8), ALU.is_equal)
-    ts(MAT(BP), R("gi"), COL(GCOL), ALU.is_equal, ZS, ALU.mult)
-    ts(R("math", 0, 128), R("gi"), COL(GCOL), ALU.is_equal)
-    ts(R("wb"), R("lane", 0, 144), COL(C15), ALU.is_equal)
-    cp(R("mh"), R("mb"))
-    act(COL(A16), COL(RCOL), scale=1.0 / (16.0 * U * ZS))
-    act(MAT(BN), MAT(BP), scale=-1.0)
-    act(MAT(BH), MAT(BP), scale=1.0 / (16.0 * U * ZS))
-    act(MAT(DR), MAT(ID), scale=COL(A16))
+    act(COL(SG), COL(RCOL), scale=-2.0, bias=1.0)
+    act(COL(HCOL), COL(P64), scale=-1.0, bias=COL(PCOL))
+    act(COL(PB), COL(RCOL), scale=4096.0, bias=2048.0)
+    act(COL(P4), COL(PCOL), bias=-4.0)
+    act(COL(EB), COL(HCOL), scale=2.0, bias=TAG)
+    act(COL(EB + 1), COL(HCOL), scale=2.0, bias=TAG + K)
+    act(COL(P4 + 1), COL(GCOL), bias=-4.0)
+    for i, val in ((NI, -1.0), (UI, U)):
+        act(MAT(i), MAT(ID), scale=val)
+    act(COL(S1), COL(S2), bias=2048.0)
+    act(COL(SG), COL(SG), scale=COL(T1))
+    for i, val in ((C0, 2048), (PM0, int(M0)), (NM0, -int(M0)), (CH, -int(XH)), (C2, 2048 - 65536)):
+        iota(ROW(i), [[0, 128]], val, 0)
+    iota(R("zero"), [[0, K]], 0, 0)
+    for i, val in ((DE, 1.0), (NE, -1.0), (SE, 1.0 / 2048)):
+        o = PAIR(i)
+        add("g", lambda q, o=o, val=val: q.affine_select(o[0], T.zero[:], [[64, 2], [0, 2], [1, 64]], ALU.not_equal, val, 0, -1),
+            [o], [R("zero")])
 
-    def lists(c, win, bank):
-        cp(R("t16"), IX(win, R("gq", 16 * c, 16 * c + 16)))
-        for h in range(2):
-            mm(PS(bank, 128 * h, 128 * h + 128),
-               [(R("mh", 144 * h + 8 - 8 * b, 144 * h + 136 - 8 * b), R("t16", b, K, 2)) for b in range(2)])
+    def layout(x):
+        for j in range(2):
+            mm(PS(6, 64 * j, 64 * j + 64),
+               [(R("mb", 144 * j + 8 - 8 * b, 144 * j + 136 - 8 * b), R("t16", x * N + b, x * N + N, 2)) for b in range(2)])
 
-    cp(R("gq", 0, 32), R("gp", 0, 32))
-    ts(R("nm"), R("jm"), COL(RCOL), ALU.not_equal, -2.0 if OPT["put"] == "a" else 2.0 ** 42, ALU.mult)
-    at = [(0, 0), (0, K), (1, 0), (1, K), (2, 0), (3, 0), (4, 0), (6, 0)]
+    def columns(out, n):
+        mm(out, [(R("o2", parts=2), R("lc", 0, n, parts=2))], last=False)
 
-    def block(blk):
-        mm(PS(at[blk][0], at[blk][1], at[blk][1] + K), [(MAT(ID), R("lane")), (MAT(UI), R("bs", K * blk, K * blk + K))])
-
-    block(0)
-    block(1)
-    lists(0, R("fav"), 5)
-    ts(COL(TF, n=2), R("tm", 0, 2), 0.5, ALU.add)
-    cp(R("gq", 32, 64), R("gp", 32, 64))
-    ts(COL(HI, n=2), COL(TF, n=2), M6, ALU.add, M6, ALU.subtract)
-    cp(R("tu"), PS(5, 0, K))
-    tt(COL(LO, n=2), COL(TF, n=2), COL(HI, n=2), ALU.subtract)
-    act(R("bu", 0, K), R("bs", 0, K), scale=U)
-    act(PS(7, K, V), R("bs", 0, K), scale=U, bias=-20480.0)
-    for blk in range(1, 8):
-        if blk > 1:
-            block(blk)
-        if blk == 1:
-            act(R("kb", 0, K), PS(0, 0, K), bias=-18432.0)
-            cp(R("s16", 0, K), R("sr", 0, K))
-        if blk == 3:
-            act(MAT(DHI), MAT(ID), scale=COL(HI))
-            act(MAT(DLO), MAT(ID), scale=COL(LO))
-        if blk % 2:
-            for b in (blk - 1, blk):
-                w, p = R("W", K * b, K * b + K), PS(at[b][0], at[b][1], at[b][1] + K)
-                if b in (2, 3, 5, 7):
-                    ts(w, p, float(K * b), ALU.add)
-                else:
-                    act(w, p, bias=float(K * b))
-
-    def sources(t, step):
-        o = (t % C) * K
-        if t < 0:
-            return
+    def block(x, b, bank, step):
+        p, w = PS(bank, 0, V), R("W", x * WN + V * b, x * WN + V * b + V)
         if step == 0:
-            ts(R("si"), R("k3"), 2047, ALU.bitwise_and)
-        elif t >= RO - C:
-            if step == 1:
-                cp(R("sf", o, o + K), R("si"))
-                store("s", T.ys[:, o:o + K], R("sf", o, o + K))
-        elif step == 1:
-            cp(R("s16", o, o + K), R("si"))
+            columns(p, V)
+            mm(p, [(RH("mat", x, 128 * (UE + x), 128 * (UE + x + 1)), RH("bs", x, V * b, V * b + V))], first=False)
+        elif b % 2:
+            ts(w, p, WT + V * b, ALU.add)
         else:
-            tt(R("ko", o, o + K), PS(7, K, V), R("si"), ALU.add)
+            act(w, p, bias=WT + V * b)
 
-    for t in range(RO):
+    def states(x, a, b):
+        cp(RH("gs", 0, 64 * x + a, 64 * x + b), RH("gp", 0, 64 * x + a, 64 * x + b))
+        cp(RH("gs", 1, 64 * x + a, 64 * x + b), RH("gp", 1, 64 * x + a + 8, 64 * x + b + 8))
+
+    def first_keys(x, c, bank, step):
+        at = (2 * x + c) * N
+        if step == 0:
+            columns(PS(bank, 0, N), N)
+            mm(PS(bank, 0, N), [(MAT(UI), R("bo", at, at + N))], first=False)
+            mm(PS(bank, N, K), [(ROW(CX), ONE), (MAT(UI), R("bo", at, at + N))])
+        if step == 1:
+            act(R("kb", at, at + N), PS(bank, 0, N), bias=COL(EB + c))
+        if step == 2:
+            tt(R("ko", at, at + N), PS(bank, N, K), R("sr", at, at + N), ALU.add)
+
+    def first_sources(x, c):
+        at = (2 * x + c) * N
+        cp(R("s16", at, at + N), R("sr", at, at + N))
+
+    def thresholds(x, step):
+        if step == 0:
+            ts(COL(TF + x), R("tm", 4 * x, 4 * x + 1), -2032.0, ALU.add)
+        else:
+            ts(MAT(DT + x, name="math"), MAT(ID), COL(TF + x), ALU.mult)
+
+    def count(x, src, step):
+        v = R("av", 8 * x + 4, 8 * x + 5)
+        if step == 0:
+            ts(v, src, COL(S1), ALU.add, COL(S2), ALU.subtract)
+        else:
+            ts(MAT(EV + x, name="math"), MAT(SEL, name="matf"), v, ALU.mult)
+
+    def first_lists(x):
+        cp(R("t16", x * N, x * N + N), IX(R("fav", NS * x, NS * x + NS), R("gs", 64 * x, 64 * x + 8)))
+
+    states(0, 0, 24)
+    for b in range(4):
+        block(0, b, b, 0)
+        block(0, b, b, 1)
+        if b == 1:
+            ts(R("wb"), R("lane", 0, 144), COL(C15), ALU.is_equal)
+            for x in range(2):
+                ts(R("av", 8 * x + 4, 8 * x + 5), COL(RCOL), 0.0, ALU.is_equal, -15.5, ALU.mult)
+    first_lists(0)
+    layout(0)
+    first_sources(0, 0)
+    ts(MAT(SEL, name="matf"), GI, COL(GCOL), ALU.is_equal, COL(SG), ALU.mult)
+    cp(R("tu", 0, N), PS(6, 0, N))
+    for i, val in ((BN, -1.0), (BKS, 1.0 / (ZS * 2048)), (NKS, -1.0 / (ZS * 2048))):
+        act(MAT(i), MAT(BP), scale=val)
+
+    def constants(step):
+        if step == 0:
+            fill(R("step"), TAG)
+            thresholds(0, 0)
+            count(0, None, 1)
+            fill(R("step", step=8), 2.0 ** 26)
+            thresholds(0, 1)
+            ts(ROW(RR), R("jm", 0, 128, parts=1), -1.0 / 2048, ALU.mult, -15.0 / 4096, ALU.add)
+        if step == 2:
+            act(MAT(BB), MAT(BP), scale=4096.0)
+        if step == 1:
+            ts(COL(TF + 2, 8), R("tm", 8, 9, parts=8), 0.5 - 16 * XH, ALU.add)
+            ts(MAT(BK5, name="matf"), GI4, COL(G4), ALU.is_equal, 0.5, ALU.mult)
+            ts(COL(HI, 8), COL(TF + 2, 8), M7, ALU.add, M7, ALU.subtract)
+            for h in range(2):
+                ts(MAT(BES + h), GI4, COL(P4 + 1 if h else GCOL), ALU.is_equal, 1.0 / 2048, ALU.mult)
+            tt(COL(LO, 8), COL(TF + 2, 8), COL(HI, 8), ALU.subtract)
+            ts(R("nm"), R("jm"), COL(RCOL), ALU.not_equal, -2.0 ** 44, ALU.mult)
+            for x in range(2):
+                ts(MAT(MGH + x, 8), R("gi", 128, 256, parts=8), COL(P4 if x else PCOL, 8), ALU.is_equal, COL(HI, 8), ALU.mult)
+                ts(MAT(MGL + x, 8), R("gi", 128, 256, parts=8), COL(P4 if x else PCOL, 8), ALU.is_equal, COL(LO, 8), ALU.mult)
+
+    def tables(x):
+        states(x, 32, 56)
+        cp(R("gq", 64 * x, 64 * x + 32), R("gp", 64 * x, 64 * x + 32))
+        cp(R("L", x * NS, x * NS + NS), R("fav", x * NS, x * NS + NS))
+
+    ready = {"tables": tables, "constants": constants, "keys": first_keys, "block": lambda b, bank, step: block(1, b, bank, step),
+             "states": states, "lists": first_lists, "layout": layout, "origins": first_sources, "thresholds": thresholds,
+             "tile": lambda: cp(R("tu", N, K), PS(6, 0, N))}
+
+    def steps(n):
+        x, t = n % 2, n // 2
         c = t % C
-        o, v = c * K, (c ^ 1) * K
+        o, s = c * K, x * N
+        m, r = (2 * x + c) * N, (2 * x + 1 - c) * N
         d = 1 + t % (NR - 1)
-        last = t == RO - 1
-        Ww = R("W")
-        inround = OPT["src"] == "round"
+        last, final = t == RO - 1, t >= RO - C
+        Ww, Lw = R("W", x * WN, x * WN + WN), R("L", x * NS, x * NS + NS)
+        Z, Z2, Z3, HS, AS = PS(4, 0, N), PS(5, 0, N), PS(5, N, K), PS(0, 0, N), PS(1, 0, 2)
+        CST, X2 = R("cst"), PS(5, K, K + N)
+        rows = slice(HP * x, HP * x + HP)
 
-        def gather(j):
-            a, b = CH[j]
-            a = max(a, DVL)
-            act(R("far", 16 * a, 16 * b), IX(Ww, R("s16", o + a, o + b)), func=ACT.Copy)
+        def S(name, a=0, b=N, w=1, step=1):
+            return R(name, w * (s + a), w * (s + b), step)
 
-        def sub(j, bank0):
-            a, b = CH[j]
-            n = b - a
-            old = R("bu", o + a, o + b) if t < C else R("x3", (t - C) * K + a, (t - C) * K + b)
+        def M(name):
+            return R(name, m, m + N)
+
+        def told(k=n):
+            return R("x3", k * N, k * N + N)
+
+        def out(eng, dst, col, name, at, ext=None):
+            for h in range(2):
+                store(eng, dst[rows, col + h * N:col + h * N + N], RH(name, h, at, at + N), ext=ext)
+
+        parts = [(ND, N, 0, 8), (ND, N, 8, 16)] if n else [(0, 64, 0, 16), (64, N, 0, 16)]
+
+        def old(a, b):
+            return R("bo", m + a, m + b) if t < C else R("x3", (n - 2 * C) * N + a, (n - 2 * C) * N + b)
+
+        def far(j):
+            a, b = parts[j][:2]
+            act(S("far", a, b, 16), IX(Ww, R("s16", m + a, m + b)), scale=1.0 / U, bias=128.0 - (WT + 1024.0) / U)
+
+        def far_v():
+            tt(S("far", 0, ND, 16), IX(Ww, R("s16", m, m + ND)), REP(m), ALU.subtract)
+
+        def place(j, p):
+            a, b, p0, p1 = parts[j]
+            return 1024 * j + 512 + (p - (p0 + p1) // 2) * (b - a), 16 * (s + a) + p * (b - a)
+
+        def sub(j):
+            a, b, p0, p1 = parts[j]
+            for p in range(p0, p1):
+                at = place(j, p)[0]
+                mm(R("ps", at, at + b - a), [(MAT(NI), old(a, b)), (MAT(ID), R("far", 16 * (s + a) + p, 16 * (s + b), 16))])
+
+        def absolute(j):
+            (q0, a0), (q1, a1) = place(j, parts[j][2]), place(j, parts[j][3])
+            act(R("ad", a0, a1), R("ps", q0, q1), func=ACT.Abs, scale=ZS)
+
+        def abs_v():
+            act(S("ad", 0, ND, 16), S("far", 0, ND, 16), func=ACT.Abs, scale=ZS / U)
+
+        def red_v():
+            mm(PS(4, 0, ND), [(R("wb", 15 - p, 143 - p), R("ad", 16 * s + p, 16 * (s + ND), 16)) for p in range(16)], first=False)
+
+        def seed():
+            act(R("seed", m, m + ND), old(0, ND), scale=U, bias=X0 + WT + 1024.0)
+
+        def repeat():
             for p in range(16):
-                at = 512 * bank0 + p * n
-                mm(R("ps", at, at + n), [(MAT(NI), old), (MAT(ID), R("far", 16 * a + p, 16 * b, 16))])
+                to, of = REP(m, p), R("seed", m, m + ND)
+                add("g", lambda q, to=to, of=of: q.affine_select(to[0], of[0], [[0, ND]], ALU.is_ge, 0.0, 0, 0), [to], [of])
 
-        def absd(j, bank0, p0, p1):
-            a, b = CH[j]
-            n = b - a
-            act(R("ad", 16 * a + p0 * n, 16 * a + p1 * n), R("ps", 512 * bank0 + p0 * n, 512 * bank0 + p1 * n),
-                func=ACT.Abs, scale=ZS, bias=-1024.0 * ZS)
+        def limits():
+            pairs = [(ROW(C0 if t < C else C2), R("cst", parts=1)), (MAT(DT + x, name="math"), CST), (MAT(EV + (x if t else 0), name="math"), CST)]
+            if t >= C:
+                pairs += [(MAT(BB), M("sg"))]
+            mm(Z, pairs, last=False)
 
-        def red(j, p0, p1):
-            a, b = CH[j]
-            n = b - a
-            gj = [i for i, (ga, gb) in enumerate(TG) if ga <= a < gb][0]
-            pairs = [(MAT(DHI), R("cst", 0, n)), (MAT(DLO), R("cst", 0, n))] if p0 == 0 else []
-            pairs += [(R("wb", 15 - p, 143 - p), R("ad", 16 * a + p * n, 16 * a + (p + 1) * n)) for p in range(p0, p1)]
-            mm(PS(4 + gj, a - TG[gj][0], b - TG[gj][0]), pairs, first=p0 == 0, last=p1 == 16)
+        def red(j):
+            a, b, p0, p1 = parts[j]
+            mm(PS(4, a, b), [(R("wb", 15 - p, 143 - p), R("ad", place(j, p)[1], place(j, p + 1)[1])) for p in range(p0, p1)],
+               first=False, last=j == 1 and n == 0)
 
-        def scan(h):
-            so, d0, d1 = R("sc", 1024 * h, 1024 * h + 1024), R("step"), R("yb", 1024 * h, 1024 * h + 1024)
+        def low(a, b):
+            ts(S("ya", a, b, 8), IX(Ww, R("tu", s + a // 2, s + b // 2)), -8 * TAG, ALU.add)
+
+        def low_a(a, b):
+            act(S("ya", a, b, 8), IX(Ww, R("tu", s + a // 2, s + b // 2)), bias=-8 * TAG)
+
+        def high(a, b):
+            tt(S("yb", a, b, 8), IX(Ww, R("tu", s + 64 + a // 2, s + 64 + b // 2)), S("ya", a, b, 8), ALU.min)
+
+        def scan(a=0, b=N):
+            so, d0, d1 = S("sc", a, b, 8), R("step", 0, 8 * (b - a)), S("yb", a, b, 8)
             add("v", lambda q: q.tensor_tensor_scan(so[0], d0[0], d1[0], 0.0, ALU.add, ALU.min), [so], [d0, d1])
 
-        def capped(j):
-            a, b = TG[j]
-            tt(PS(7, a, b), R("sc", 8 * a + 7, 8 * b, 8), R("kb", a, b) if t == 0 else PS(6, o + a, o + b), ALU.min)
-
-        def lapsed(j):
-            a, b = TG[j]
-            tt(R("u1", a, b), PS(4 + j, 0, b - a), R("ko", o + a, o + b), ALU.max)
-
-        def favoured(j):
-            a, b = TG[j]
-            tt(PS(7, a, b), PS(7, a, b), R("u1", a, b), ALU.min)
-
-        def number(j):
-            a, b = TG[j]
-            ts(R("x2", a, b), PS(7, a, b), M16, ALU.add, M16, ALU.subtract)
-
-        def cuts(j, early):
-            a, b = TG[j]
-            n = b - a
-            if early:
-                pairs = [(MAT(BP), R("bu", o + a, o + b)), (MAT(MGH, 8), R("cst", 0, n, parts=8)), (MAT(MGL, 8), R("cst", 0, n, parts=8))]
-                if t > 0:
-                    pairs += [(MAT(BN), R("bu", v + a, v + b)), (MAT(BP), R("x3", (t - 1) * K + a, (t - 1) * K + b))]
-            else:
-                pairs = [(MAT(BN), R("x2", a, b))]
-            mm(PS(ZB[j], K, K + n), pairs, first=early, last=not early)
-
-        def direct(j, step):
-            a, b = TG[j]
-            if step == 0:
-                if last:
-                    ts(R("x2u", a, b), R("x2", a, b), 1.0 / U, ALU.mult)
-            elif step == 1:
-                tt(PS(ZB[j], 0, b - a), PS(ZB[j], K, K + b - a), R("bs" if last else "bu", o + a, o + b), ALU.min)
-            else:
-                tt(R("x3", t * K + a, t * K + b), PS(ZB[j], 0, b - a), R("x2u" if last else "x2", a, b), ALU.max)
-
-        def keys(j, step):
-            a, b = TG[j]
-            if step == 0:
-                tt(R("fb", a, b), PS(ZB[j], K, K + b - a), R("kb", o + a, o + b), ALU.min)
-            elif step == 1:
-                tt(R("k3", a, b), PS(7, a, b), R("fb", a, b), ALU.max)
-            else:
-                ts(R("x3", t * K + a, t * K + b), R("k3", a, b), M16, ALU.add, M16, ALU.subtract)
-
-        def putv(j):
-            a, b = TG[j]
-            if OPT["put"] == "v":
-                tt(R("put", a, b), PS(ZB[j], K, K + b - a), R("nm", a + t, b + t), ALU.is_gt)
-
-        def hsum(early):
-            mm(PS(HB, 0, K), [(MAT(DR), R("cst")) if early else (MAT(BH), R("y0"))], first=early, last=not early)
-
-        def chosen(step):
-            if step == 0:
-                tt(R("eq"), PS(HB, 0, K), R("j2"), ALU.is_equal)
-            else:
-                tt(R("sel"), IX(R("L"), R("gq", 32 + 16 * c, 48 + 16 * c)), R("eq"), ALU.mult)
-                mm(PS(2, K, V), [(R("math", 128, 256), R("t16")), (R("math", 0, 128), R("sel"))])
-
-        HB = 0
-        ZB = (4, 1)
-        if DVL:
-            cp(R("far", 0, 16 * DVL), IX(Ww, R("s16", o, o + DVL)))
-        gather(0)
-        for h in range(2):
-            ts(R("ya", 1024 * h, 1024 * h + 1024), IX(Ww, R("tu", 64 * h, 64 * h + 64)), -16384.0, ALU.add)
-        sub(0, 0)
-        gather(1)
-        sub(1, 2)
-        for h in range(2):
-            tt(R("yb", 1024 * h, 1024 * h + 1024), IX(Ww, R("tu", 128 + 64 * h, 192 + 64 * h)), R("ya", 1024 * h, 1024 * h + 1024), ALU.min)
-        absd(0, 0, 0, 16)
-        red(0, 0, 16)
-        gather(2)
-        sub(2, 0)
-        absd(1, 2, 0, 16)
-        red(1, 0, 16)
-        gather(3)
-        scan(0)
-        if inround:
-            sources(t - 1, 0)
-        if t == 0:
-            tt(R("ko", 0, K), PS(7, K, V), R("sr", 0, K), ALU.add)
-            ts(MAT(MGH, 8), MAT(E8, 8), COL(HI + 1, 8), ALU.mult)
-            ts(MAT(MGL, 8), MAT(E8, 8), COL(LO + 1, 8), ALU.mult)
-        lapsed(0)
-        capped(0)
-        cuts(0, True)
-        sub(3, 2)
-        favoured(0)
-        if inround:
-            sources(t - 1, 1)
-        if t == 0:
-            cp(R("L"), R("fav"))
-        number(0)
-        cuts(0, False)
-        scan(1)
-        absd(2, 0, 0, 16)
-        red(2, 0, 16)
-        cuts(1, True)
-        absd(3, 2, 0, 12)
-        red(3, 0, 12)
-        absd(3, 2, 12, 16)
-        red(3, 12, 16)
-        hsum(True)
-        a1, b1 = TG[1]
-        if last:
-            direct(0, 0)
-            direct(0, 1)
-            capped(1)
-            direct(0, 2)
-            ts(R("xm"), PS(7, a1, b1), M16, ALU.add, M16, ALU.subtract)
-        else:
-            keys(0, 0)
-            capped(1)
-            keys(0, 1)
-            ts(R("xm"), PS(7, a1, b1), M16, ALU.add, M16, ALU.subtract)
-            keys(0, 2)
-        send(t, 0)
-        putv(0)
-        if OPT["h"] == "a":
-            act(R("i1"), R("ya", 7, 2048, 8), bias=M16)
-            act(R("y0"), R("i1"), bias=-M16)
-        else:
-            ts(R("y0"), R("ya", 7, 2048, 8), M16, ALU.add, M16, ALU.subtract)
-        old = R("bu", o + a1, o + b1) if t < C else R("x3", (t - C) * K + a1, (t - C) * K + b1)
-        tt(PS(5, 128, 256), PS(5, 0, 128), old, ALU.max)
-        hsum(False)
-        tt(R("x2", a1, b1), PS(5, 128, 256), R("xm"), ALU.min)
-        cuts(1, False)
-        if inround and not last:
-            sources(t - 1, 2)
-        if t == 0:
-            cp(R("s16", K, V), R("sr", K, V))
-        if OPT["h"] == "v":
-            ts(R("j2"), PS(HB, 0, K), M0, ALU.add, M0, ALU.subtract)
-        for s in range(3):
-            direct(1, s)
-        send(t, 1)
-        if OPT["h"] == "a":
-            act(R("j1"), PS(HB, 0, K), bias=M0)
-            act(R("j2"), R("j1"), bias=-M0)
-        act(R("t32"), IX(R("L"), R("gq", 16 * c, 16 * c + 16)), func=ACT.Copy)
-        if last:
-            store("s", T.yx[:, o:o + K], R("x3", t * K, t * K + K))
-        if OPT["put"] == "v":
-            chosen(0)
-            putv(1)
-            chosen(1)
-        if last:
-            keys(0, 0)
-        keys(1, 0)
-        if OPT["put"] == "a" or not last:
-            act(R("sg"), R("fb"), func=ACT.Sign, bias=2.0 ** 20, acc=None if last else COL(ACC))
-        if OPT["put"] == "a":
-            mm(PS(3, 0, K), [(MAT(ID), R("nm", t, t + K)), (MAT(ID), R("sg"))])
-            act(R("put"), PS(3, 0, K), func=ACT.Relu)
-            chosen(0)
-            lapsed(1)
-            chosen(1)
-        else:
-            lapsed(1)
-        if last:
-            keys(0, 1)
-        favoured(1)
-        keys(1, 1)
-        if not last:
-            mm(PS(5, K, V), [(MAT(ID), R("lane")), (MAT(ID), R("x3", t * K, t * K + K))])
-            blk = 2 * d + c
-            act(PS(4, 0, K), R("lane"), bias=float(K * blk))
+        def known():
+            pairs = [(MAT(MGH + x, 8), R("cst", parts=8)), (MAT(MGL + x, 8), R("cst", parts=8))]
             if t == 0:
-                act(PS(6, 0, V), R("W", 0, V), bias=-18432.0)
-                act(R("kb", K, V), R("W", K, V), bias=-18432.0)
-            act(R("W", o, o + K), PS(5, K, V), bias=float(o))
-        tt(R("ee"), PS(2, K, V), R("put"), ALU.mult)
-        if last or not inround:
-            sources(t, 0)
-        pd = 1 + (t - 1) % (NR - 1)
-        tt(IX(R("L"), R("gq", 16 * c, 16 * c + 16)), R("t32"), R("ee"), ALU.add)
-        if last:
-            store("s", T.yl[:], R("L"))
-            sources(t, 1)
-            act(R("outb", (t - 1) * K, t * K), R("land", (t - 1) * K, t * K), scale=1.0 / U, ext=arrived(t - 1))
-            store("a", T.yx[:, pd * V + v:pd * V + v + K], R("outb", (t - 1) * K, t * K))
-            store("a", T.yx[:, d * V + o:d * V + o + K], R("land", t * K, t * K + K), ext=arrived(t))
-            break
-        if t < RO - C:
-            act(PS(7, K, V), R("x3", t * K, t * K + K), bias=-20480.0)
-        if t == 0:
-            act(R("bu", K, V), R("bs", K, V), scale=U)
-            act(PS(3, K, V), R("bs", K, V), scale=U, bias=-20480.0)
-        a, b = TG[0]
-        if not OPT["one"]:
-            tt(R("W", K * blk + a, K * blk + b), PS(4, a, b), R("land", t * K + a, t * K + b), ALU.add, ext=arrived(t, 0))
-        lists(c ^ 1, R("L"), 0)
-        act(COL(AP_), COL(ACC), scale=0.5, bias=COL(AP_))
-        act(COL(GG), COL(ACC), scale=0.5, bias=COL(GG))
-        act(COL(T1), COL(AP_), bias=M5)
-        if t > 0:
-            act(R("outb", (t - 1) * K, t * K), R("land", (t - 1) * K, t * K), scale=1.0 / U, ext=arrived(t - 1))
-            store("s", T.yx[:, pd * V + v:pd * V + v + K], R("outb", (t - 1) * K, t * K))
-        act(COL(T2), COL(T1), bias=-M5)
-        if t == RO - C:
-            act(R("outb", (RO - 1) * K, RO * K), R("x3", t * K, t * K + K), scale=1.0 / U)
-            store("s", T.yx[:, o:o + K], R("outb", (RO - 1) * K, RO * K))
-        act(COL(CC), COL(T2), scale=-1.0, bias=COL(GG))
-        act(MAT(DLO), MAT(ID), scale=COL(CC))
-        if t == 0:
-            tt(R("ko", K, V), PS(3, K, V), R("sr", K, V), ALU.add)
-        if not inround:
-            sources(t, 1)
-            sources(t, 2)
-        cp(R("tu"), PS(0, 0, K))
-        a, b = (0, K) if OPT["one"] else TG[1]
-        tt(R("W", K * blk + a, K * blk + b), PS(4, a, b), R("land", t * K + a, t * K + b), ALU.add, ext=arrived(t, 1))
+                pairs += [(MAT(BP), M("bo"))]
+            else:
+                pairs += [(MAT(BN if c else BP), S("gap")), (MAT(BP), told(n - 2))]
+            return pairs
 
-    emit(ops, queue, T, nsent[0])
+        def cuts():
+            mm(Z2, known(), last=False)
+
+        def lapsed():
+            tt(Z, Z, M("ko"), ALU.max)
+
+        def based():
+            tt(Z, Z, M("kb"), ALU.min)
+
+        def least():
+            tt(S("k2"), Z, R("sc", 8 * s + 7, 8 * (s + N), 8), ALU.min)
+
+        def number():
+            ts(S("x2h"), S("k2"), 1.0 / U, ALU.mult, XH + 128 - 0.140625, ALU.add)
+            mm(Z2, [(MAT(BN), S("x2h"))], first=False)
+            mm(X2, [(ROW(CH), ONE), (MAT(ID), S("x2h"))])
+
+        def denied():
+            tt(S("back"), Z2, M("bo"), ALU.min)
+
+        def tell():
+            tt(told(), X2, S("back"), ALU.max)
+            send(n)
+            if final:
+                out("s", T.yx, o, "x3", n * N)
+
+        def reset(step):
+            if final and step == 0:
+                tt(Z, Z2, M("kb"), ALU.min)
+            if final and step == 1:
+                tt(S("k2"), Z, S("k2"), ALU.max)
+
+        def row():
+            mm(Z3, [(MAT(ID), R("nm", t, t + N)), (MAT(BN), S("x2h")), (MAT(BP), told())])
+
+        def first():
+            ts(S("h0"), R("ya", 8 * s + 7, 8 * (s + N), 8), 1.0 / U, ALU.mult, XH + 128, ALU.add)
+
+        def entry():
+            mm(HS, [(ROW(RR), ONE), (MAT(BKS), S("h0")), (ROW(PM0), ONE), (ROW(NM0), ONE), (MAT(NKS), S("h0"))])
+
+        def pick():
+            act(S("pick"), HS, func=ACT.Relu, scale=65536.0 * 128, bias=COL(PB))
+
+        def chosen():
+            at = 64 * x + 32 + 16 * c
+            tt(S("sel"), IX(Lw, R("gs", at, at + 8)), S("pick"), ALU.min)
+
+        def put():
+            act(M("sg"), Z3, func=ACT.Sign, bias=(16 * XH - 0.5) * ZS, acc=None if last else R("av", 8 * x, 8 * x + 1))
+
+        def merge():
+            for h in range(2):
+                mm(PS(6, K + h * N, K + h * N + N), [(MAT(SE + h), S("t16")), (MAT(NE + h), M("sg"))])
+                mm(PS(6, h * N, h * N + N), [(MAT(BES + h), S("sel")), (MAT(DE + h), M("sg"))])
+
+        def counted():
+            if not last:
+                mm(AS, [(MAT(BK5, name="matf"), R("av", 8 * x, 8 * x + 2)), (MAT(SEL, name="matf"), R("av", 8 * x + 4, 8 * x + 6))])
+
+        def ab():
+            act(R("ab"), PS(6, 0, V), func=ACT.Relu, scale=2048.0, bias=-2048.0)
+
+        def edit():
+            at = 64 * x + 16 * c
+            tt(IX(Lw, R("gq", at, at + 16)), R("ab", 0, K), R("ab", K, V), ALU.add)
+            if last:
+                store("a", T.yl[rows, :], RH("L", 0, x * NS, x * NS + NS))
+
+        def window(step, name, col, bank, ext=None):
+            if last:
+                return
+            if step == 0:
+                columns(PS(bank, 0, K), K)
+                for h in range(2):
+                    mm(PS(bank, h * N, h * N + N), [(MAT(UE + h), R(name, n * N, n * N + N))], first=False, last=h == 1, ext=ext)
+            else:
+                act(R("W", x * WN + col, x * WN + col + K), PS(bank, 0, K), bias=WT + col)
+
+        def own(step):
+            window(step, "x3", o, 7)
+
+        def copies(step):
+            window(step, "land", d * V + o, 2, arrived(n))
+
+        def keep():
+            out("s", T.yx, d * V + o, "land", n * N, arrived(n))
+
+        def source():
+            ts(S("si"), S("k2"), 2047, ALU.bitwise_and)
+
+        def sources():
+            cp(M("sf" if final else "s16"), S("si"))
+            if final:
+                out("s", T.ys, o, "sf", m)
+
+        def aged():
+            if not final:
+                ts(M("ko"), S("k2"), ~(63 << 11), ALU.bitwise_and)
+
+        def tally(step):
+            if not last:
+                count(x, PS(1, 0, 1), step)
+
+        def other(step):
+            if t == 0:
+                first_keys(x, 1, 7, step)
+                if step == 0:
+                    first_sources(x, 1)
+                if step == 2:
+                    tt(S("gap"), M("bo"), R("bo", r, r + N), ALU.subtract)
+
+        def grantors():
+            if not last:
+                at = 64 * x + 16 - 16 * c
+                cp(S("t16"), IX(Lw, R("gs", at, at + 8)))
+
+        def lay():
+            if not last:
+                layout(x)
+
+        def offsets():
+            if not last:
+                cp(S("tu"), PS(6, 0, N))
+
+        return {"far_v": far_v, "abs_v": abs_v, "red_v": red_v, "seed": seed, "repeat": repeat,
+                "far": far, "sub": sub, "abs": absolute, "limits": limits, "red": red, "low": low, "low_a": low_a, "high": high,
+                "scan": scan, "cuts": cuts, "lapsed": lapsed, "based": based, "least": least, "number": number, "counted": counted,
+                "denied": denied, "tell": tell, "reset": reset, "row": row, "first": first, "entry": entry, "pick": pick,
+                "chosen": chosen, "put": put, "merge": merge, "ab": ab, "edit": edit, "own": own, "copies": copies,
+                "keep": keep, "source": source, "sources": sources, "aged": aged, "tally": tally, "other": other,
+                "grantors": grantors, "lay": lay, "offsets": offsets}
+
+    order = [s.split() for s in ORDER.split(",")]
+    turns = {n: steps(n) for n in range(2 * RO)}
+    for name, *args in [s.split() for s in OPENING.split(",")]:
+        dict(turns[name.count(">")], **ready)[name.lstrip(">")](*[int(a) for a in args])
+    closing = [[s.split() for s in c.split(",")] for c in CLOSING]
+    for n in range(1, 2 * RO + 1):
+        for name, *args in (closing[n - 2 * RO + 1] if n >= 2 * RO - 1 else order):
+            table = turns.get(n - name.count("<") + name.count(">"), {})
+            if name.lstrip("<>") in table:
+                table[name.lstrip("<>")](*[int(a) for a in args])
+
+    emit(ops, queue, T, 2 * RO * neng)
 
 
 def emit(ops, queue, T, nsent):
     def meet(xs, ys):
-        return any(x[0] == y[0] and x[1] < y[2] and y[1] < x[2] for x in xs for y in ys)
+        return any(x[0] == y[0] and x[1] < y[2] and y[1] < x[2] and x[3] < y[4] and y[3] < x[4] for x in xs for y in ys)
 
     def banks(x):
         s = set()

from concourse.mybir import AluOpType, ActivationFunctionType

ALU = AluOpType
ACT = ActivationFunctionType
K, C, NS, RO, NR = 256, 2, 384, 6, 4
V, WN = C * K, NR * C * K
N = K // 2
ND = 52
HP = 64
U = 2.0 ** 17
TAG = 2048.0
X0 = -128.0 * U
WT = 10 * TAG
M0 = 1.5 * 2.0 ** 16
M5 = 1.5 * 2.0 ** 28
M7 = 1.5 * 2.0 ** 30
XH = 1280.0
ZS = 2.0 ** 27

ORDER = """
<cuts, <number, <<offsets, <<tally 1, far 0, <denied, low_a 0 128, <<other 2, <chosen, sub 0, <tell, <row, far_v, >>repeat,
<reset 0, abs 0, sub 1, <own 0, <put, <reset 1, limits, high 0 128, <source, <merge, abs 1, red 0, abs_v, <own 1, red 1,
first, <ab, entry, pick, <aged, red_v, <copies 0, <keep, <copies 1, >>>seed, <other 0, scan,
lapsed, <edit, <sources, based, <counted, <grantors, least, <tally 0, <lay, <other 1"""
OPENING = """
far 0, keys 0 0 4 0, low 0 80, low_a 80 128, block 0 6 0, block 1 7 0, block 2 5 0, sub 0, constants 0, tables 0, far 1,
keys 0 0 4 1, >seed, >repeat, >>seed, >>repeat, >>>seed, high 0 128, sub 1, abs 0, first, keys 0 0 4 2, constants 1, limits, red 0, entry, block 0 6 1, states 1 0 24,
scan, block 1 7 1, block 3 7 0, lists 1, abs 1, red 1, layout 1, block 2 5 1, keys 1 0 5 0, block 3 7 1, origins 1 0, tile,
keys 1 0 5 1, pick, constants 2, thresholds 1 0, lapsed, thresholds 1 1, based, keys 1 0 5 2, least, tables 1"""
CLOSING = ["""
far 0, <cuts, <number, <<offsets, <chosen, <<tally 1, <denied, low_a 0 128, <tell, sub 0, sub 1, <row,
<reset 0, far_v, <reset 1, high 0 128, limits, abs 0, first, <source, red 0, scan, abs 1, red 1, abs_v, red_v, <put,
<merge, entry, cuts, <ab, pick, lapsed, <sources, based, <keep, least""", """
<number, <<edit, <denied, <chosen, <tell, <row, <put, <reset 0, <merge, <reset 1, <ab, <source, <keep,
<sources, <edit"""]

F, B, H, I32, U16 = "float32", "bfloat16", "float16", "int32", "uint16"
SCRATCH = {
    "ps": ("psum", [128, 4096], F),
    "W": ("sbuf", [128, 2 * WN], F),
    "bs": ("sbuf", [128, WN], B),
    "bo": ("sbuf", [128, 4 * N], B),
    "fav": ("sbuf", [128, 2 * NS], I32),
    "sr": ("sbuf", [128, 4 * N], I32),
    "gp": ("sbuf", [128, 128], I32),
    "gq": ("sbuf", [128, 128], U16),
    "gs": ("sbuf", [128, 128], U16),
    "tm": ("sbuf", [128, 12], I32),
    "ci": ("sbuf", [128, 16], I32),
    "cf": ("sbuf", [128, 80], F),
    "av": ("sbuf", [128, 16], F),
    "L": ("sbuf", [128, 2 * NS], F),
    "s16": ("sbuf", [128, 4 * N], U16),
    "tu": ("sbuf", [128, 2 * N], U16),
    "t16": ("sbuf", [128, 2 * N], H),
    "gap": ("sbuf", [128, 2 * N], B),
    "seed": ("sbuf", [128, 4 * N], F),
    "rep": ("sbuf", [128, 64 * ND], F),
    "far": ("sbuf", [128, 32 * N], B),
    "ad": ("sbuf", [128, 32 * N], B),
    "ya": ("sbuf", [128, 16 * N], F),
    "yb": ("sbuf", [128, 16 * N], F),
    "sc": ("sbuf", [128, 16 * N], F),
    "step": ("sbuf", [128, 8 * N], B),
    "kb": ("sbuf", [128, 4 * N], F),
    "ko": ("sbuf", [128, 4 * N], I32),
    "k2": ("sbuf", [128, 2 * N], I32),
    "x2h": ("sbuf", [128, 2 * N], H),
    "back": ("sbuf", [128, 2 * N], B),
    "si": ("sbuf", [128, 2 * N], I32),
    "sf": ("sbuf", [128, 4 * N], F),
    "x3": ("sbuf", [128, 2 * RO * N], B),
    "land": ("sbuf", [128, 2 * RO * N], B),
    "sg": ("sbuf", [128, 4 * N], B),
    "ab": ("sbuf", [128, V], F),
    "h0": ("sbuf", [128, 2 * N], H),
    "pick": ("sbuf", [128, 2 * N], F),
    "sel": ("sbuf", [128, 2 * N], H),
    "zero": ("sbuf", [128, K], B),
    "lane": ("sbuf", [128, K], B),
    "lc": ("sbuf", [128, V], H),
    "o2": ("sbuf", [128, 128], B),
    "gi": ("sbuf", [128, 4 * 128], B),
    "jm": ("sbuf", [128, 144], B),
    "nm": ("sbuf", [128, 144], B),
    "one": ("sbuf", [128, 144], B),
    "cst": ("sbuf", [128, N], B),
    "cr": ("sbuf", [128, 8 * 128], B),
    "mb": ("sbuf", [128, 288], B),
    "wb": ("sbuf", [128, 144], B),
    "mat": ("sbuf", [128, 22 * 128], B),
    "math": ("sbuf", [128, 4 * 128], H),
    "matf": ("sbuf", [128, 2 * 128], F),
}
ENGINES = ["g", "v", "a", "p", "s"]
NDMA = 84
SEMAPHORES = ["e_" + e for e in ENGINES] + ["d%d" % i for i in range(NDMA)] + ["arr%d" % i for i in range(2 * RO)] + ["sent"]

ID, UI, NI, BP, BN, BB, BKS, NKS = range(8)
DE, UE, NE, SE, BES, MGH, MGL = range(8, 22, 2)
DT, EV = 0, 2
BK5, SEL = range(2)
RR, PM0, NM0, C0, C2, CX, CH = range(7)


def rank_program(g, core, T, topo):
    rank = T.rank_of(core)
    if rank is None:
        return
    ops = []
    queue = {"g": g, "v": g.vector, "a": g.scalar, "p": g.tensor, "s": g.sync}

    def R(name, a=None, b=None, step=1, parts=128, at=0):
        n = T[name].shape[1]
        a = 0 if a is None else a
        b = n if b is None else b
        ap = T[name][at:at + parts, a:b:step] if step > 1 else T[name][at:at + parts, a:b]
        return (ap, [(name, a, b, at, at + parts)])

    def RH(name, h, a, b):
        return R(name, a, b, parts=HP, at=HP * h)

    def REP(m, p=None):
        at = m // N * 16 * ND
        if p is None:
            return (T.rep[:, at:at + 16 * ND], [("rep%d" % i, m, m + 1, 0, 128) for i in range(16)])
        return (T.rep[:, at + p:at + 16 * ND:16], [("rep%d" % p, m, m + 1, 0, 128)])

    def IX(win, off):
        return (win[0].indirect(off[0]), win[1], off[1])

    def PS(bank, a, b):
        return R("ps", 512 * bank + a, 512 * bank + b)

    def MAT(i, parts=128, name="mat"):
        return R(name, 128 * i, 128 * i + 128, parts=parts)

    def PAIR(i):
        return R("mat", 128 * i, 128 * i + 256)

    def ROW(i):
        return MAT(i, 1, "cr")

    def COL(i, parts=128, n=1):
        return R("cf", i, i + n, parts=parts)

    def add(eng, fn, outs, ins, dma=False, ext=None):
        rd, wr = [], []
        for o in outs:
            wr += o[1]
            if len(o) > 2:
                rd += o[2]
        for o in ins:
            if isinstance(o, tuple):
                rd += o[1]
                if len(o) > 2:
                    rd += o[2]
        ops.append({"e": eng, "fn": fn, "rd": rd, "wr": wr, "dma": dma, "ext": ext})

    def ap(o):
        return o[0] if isinstance(o, tuple) else o

    def tt(out, a, b, op):
        add("v", lambda q: q.tensor_tensor(out[0], a[0], b[0], op), [out], [a, b])

    def ts(out, a, s1, op0, s2=None, op1=None):
        if s2 is None:
            add("v", lambda q: q.tensor_scalar(out[0], a[0], ap(s1), None, op0), [out], [a, s1])
        else:
            add("v", lambda q: q.tensor_scalar(out[0], a[0], ap(s1), ap(s2), op0, op1), [out], [a, s1, s2])

    def cp(out, a):
        add("v", lambda q: q.tensor_copy(out[0], a[0]), [out], [a])

    def fill(out, val):
        add("v", lambda q: q.memset(out[0], val), [out], [])

    def act(out, a, func=ACT.Identity, bias=0.0, scale=1.0, acc=None):
        if acc is None:
            add("a", lambda q: q.activation(out[0], a[0], func, bias=ap(bias), scale=ap(scale)), [out], [a, bias, scale])
        else:
            add("a", lambda q: q.activation(out[0], a[0], func, bias=ap(bias), scale=ap(scale), accum_out=acc[0]),
                [out, acc], [a, bias, scale])

    def mm(out, pairs, first=True, last=True, ext=None):
        for j, (l, r) in enumerate(pairs):
            st, sp = first and j == 0, last and j == len(pairs) - 1
            add("p", lambda q, l=l, r=r, st=st, sp=sp: q.matmul(out[0], l[0], r[0], st, sp), [out], [l, r], ext=ext)

    def load(eng, out, src):
        add(eng, lambda q: q.dma_start(out[0], src), [out], [], dma=True)

    def store(eng, dst, src, ext=None):
        add(eng, lambda q: q.dma_start(dst, src[0]), [], [src], dma=True, ext=ext)

    def iota(out, pattern, base, cm, whole=False):
        if whole:
            add("g", lambda q: q.iota(out[0], pattern, base, cm), [out], [])
        else:
            add("g", lambda q: q.iota(out[0], pattern, base, cm, allow_small_or_imprecise_dtypes=True), [out], [])

    emask = -1
    for peer in T.cores:
        if peer != core:
            emask &= topo.mask(core, peer)
    neng = bin(emask).count("1")

    def send(n):
        dst = T.cores[(rank + 1 + n // 2 % (NR - 1)) % NR]
        rid, pid = topo.addr(dst, core)
        src, to, sem = R("x3", n * N, n * N + N), R("land", n * N, n * N + N), T.sem["arr%d" % n]
        add("g", lambda q: q.remote_dma(to[0], src[0], sem, T.sem.sent, pid, rid, emask), [], [src], dma="remote")

    def arrived(n):
        return [(T.sem["arr%d" % n], neng)]

    PCOL, RCOL, C15, TF, HI, LO, PB, S1, S2, SG, T1, EB, P4 = [4 * i for i in range(13)]
    GCOL, G4, P64, HCOL = RCOL + 1, RCOL + 2, RCOL + 3, 60
    ONE = R("one", 0, N, parts=1)
    fill(R("one"), 1.0)

    def loads(x, qa, qb):
        rows = slice(HP * x, HP * x + HP)
        for h in range(2):
            load(qb, RH("gp", h, 64 * x, 64 * x + 32), T.grant[rows, :])
        load(qa, RH("bs", x, 0, 1024), T.base[rows, 0:1024])
        load(qa, RH("bs", x, 1024, WN), T.base[rows, 1024:WN])
        for h in range(2):
            load(qb, RH("fav", h, NS * x, NS * x + NS), T.favor[rows, :])
        for h in range(2):
            load(qb, RH("sr", h, 2 * x * N, 2 * x * N + N), T.src[rows, h * N:h * N + N])
            load(qa, RH("bo", h, 2 * x * N, 2 * x * N + N), T.base[rows, h * N:h * N + N])
        for h in range(2):
            load(qb, RH("tm", h, 4 * x, 4 * x + 1), T.th[rows])
            load(qb, RH("gp", h, 64 * x + 32, 64 * x + 64), T.part[rows, :])

    def later(x):
        rows = slice(HP * x, HP * x + HP)
        for h in range(2):
            load("s", RH("bo", h, (2 * x + 1) * N, (2 * x + 2) * N), T.base[rows, K + h * N:K + h * N + N])
            load("s", RH("sr", h, (2 * x + 1) * N, (2 * x + 2) * N), T.src[rows, K + h * N:K + h * N + N])

    loads(0, "a", "s")
    load("s", R("tm", 8, 9, parts=8), T.mg[:])
    loads(1, "s", "s")
    later(0)
    later(1)

    iota(COL(PCOL), [[0, 1]], 0, 1)
    iota(R("ci", 0, 1), [[0, 1]], 0, 1, whole=True)
    iota(R("gi", 256, 512), [[64, 2], [0, 2], [1, 64]], 0, 0)
    iota(R("lane"), [[1, K]], 0, 0)
    iota(R("gi", 0, 128), [[1, 8], [0, 16]], 0, 0)
    for h in range(2):
        o, i = R("mb", 144 * h, 144 * h + 144), R("one", 0, 144)
        add("g", lambda q, o=o, i=i, h=h: q.affine_select(o[0], i[0], [[16, 9], [-1000, 2], [-1, 8]], ALU.is_equal, 0.0,
                                                          8 * h + 7 + 1000, -1), [o], [i])
    iota(R("jm"), [[0, 9], [1, 16]], 0, 0)
    iota(R("gi", 128, 256), [[0, 2], [1, 4], [0, 16]], 0, 0)
    GI, GI4, M64 = R("gi", 0, 128), R("gi", 128, 256), R("gi", 256, 512)

    fill(R("lc", parts=2), X0 / 4096)
    fill(R("o2", parts=2), 4096.0)
    ts(R("ci", 4, 5), R("ci", 0, 1), 15, ALU.bitwise_and)
    ts(R("ci", 5, 6), R("ci", 0, 1), 4, ALU.arith_shift_right)
    ts(R("ci", 6, 7), R("ci", 0, 1), 4, ALU.arith_shift_right, 3, ALU.bitwise_and)
    ts(R("ci", 7, 8), R("ci", 0, 1), 63, ALU.bitwise_and)
    fill(R("o2", parts=1), 1.0)
    cp(COL(RCOL, n=4), R("ci", 4, 8))
    cp(R("lc", 0, K, parts=1), R("lane", parts=1))
    ts(R("lc", K, V, parts=1), R("lane", parts=1), float(K), ALU.add)
    ts(PAIR(UE), M64, COL(PCOL), ALU.is_equal, U, ALU.mult)
    ts(MAT(ID), R("lane", 0, 128), COL(PCOL), ALU.is_equal)
    ts(MAT(BP), GI, COL(GCOL), ALU.is_equal, ZS, ALU.mult)
    ts(COL(S2), COL(RCOL), 1.0, ALU.is_equal, M5, ALU.mult)
    ts(COL(T1), COL(RCOL), 1.0, ALU.is_le)
    act(R("cst"), R("one", 0, N), scale=-ZS)
    act(R("av"), R("one", 0, 16), scale=0.0)
    act(ROW(CX), ONE, scale=X0)
    act(COL(C15), COL(GCOL), scale=16.0, bias=15.0)
    act(COL(SG), COL(RCOL), scale=-2.0, bias=1.0)
    act(COL(HCOL), COL(P64), scale=-1.0, bias=COL(PCOL))
    act(COL(PB), COL(RCOL), scale=4096.0, bias=2048.0)
    act(COL(P4), COL(PCOL), bias=-4.0)
    act(COL(EB), COL(HCOL), scale=2.0, bias=TAG)
    act(COL(EB + 1), COL(HCOL), scale=2.0, bias=TAG + K)
    act(COL(P4 + 1), COL(GCOL), bias=-4.0)
    for i, val in ((NI, -1.0), (UI, U)):
        act(MAT(i), MAT(ID), scale=val)
    act(COL(S1), COL(S2), bias=2048.0)
    act(COL(SG), COL(SG), scale=COL(T1))
    for i, val in ((C0, 2048), (PM0, int(M0)), (NM0, -int(M0)), (CH, -int(XH)), (C2, 2048 - 65536)):
        iota(ROW(i), [[0, 128]], val, 0)
    iota(R("zero"), [[0, K]], 0, 0)
    for i, val in ((DE, 1.0), (NE, -1.0), (SE, 1.0 / 2048)):
        o = PAIR(i)
        add("g", lambda q, o=o, val=val: q.affine_select(o[0], T.zero[:], [[64, 2], [0, 2], [1, 64]], ALU.not_equal, val, 0, -1),
            [o], [R("zero")])

    def layout(x):
        for j in range(2):
            mm(PS(6, 64 * j, 64 * j + 64),
               [(R("mb", 144 * j + 8 - 8 * b, 144 * j + 136 - 8 * b), R("t16", x * N + b, x * N + N, 2)) for b in range(2)])

    def columns(out, n):
        mm(out, [(R("o2", parts=2), R("lc", 0, n, parts=2))], last=False)

    def block(x, b, bank, step):
        p, w = PS(bank, 0, V), R("W", x * WN + V * b, x * WN + V * b + V)
        if step == 0:
            columns(p, V)
            mm(p, [(RH("mat", x, 128 * (UE + x), 128 * (UE + x + 1)), RH("bs", x, V * b, V * b + V))], first=False)
        elif b % 2:
            ts(w, p, WT + V * b, ALU.add)
        else:
            act(w, p, bias=WT + V * b)

    def states(x, a, b):
        cp(RH("gs", 0, 64 * x + a, 64 * x + b), RH("gp", 0, 64 * x + a, 64 * x + b))
        cp(RH("gs", 1, 64 * x + a, 64 * x + b), RH("gp", 1, 64 * x + a + 8, 64 * x + b + 8))

    def first_keys(x, c, bank, step):
        at = (2 * x + c) * N
        if step == 0:
            columns(PS(bank, 0, N), N)
            mm(PS(bank, 0, N), [(MAT(UI), R("bo", at, at + N))], first=False)
            mm(PS(bank, N, K), [(ROW(CX), ONE), (MAT(UI), R("bo", at, at + N))])
        if step == 1:
            act(R("kb", at, at + N), PS(bank, 0, N), bias=COL(EB + c))
        if step == 2:
            tt(R("ko", at, at + N), PS(bank, N, K), R("sr", at, at + N), ALU.add)

    def first_sources(x, c):
        at = (2 * x + c) * N
        cp(R("s16", at, at + N), R("sr", at, at + N))

    def thresholds(x, step):
        if step == 0:
            ts(COL(TF + x), R("tm", 4 * x, 4 * x + 1), -2032.0, ALU.add)
        else:
            ts(MAT(DT + x, name="math"), MAT(ID), COL(TF + x), ALU.mult)

    def count(x, src, step):
        v = R("av", 8 * x + 4, 8 * x + 5)
        if step == 0:
            ts(v, src, COL(S1), ALU.add, COL(S2), ALU.subtract)
        else:
            ts(MAT(EV + x, name="math"), MAT(SEL, name="matf"), v, ALU.mult)

    def first_lists(x):
        cp(R("t16", x * N, x * N + N), IX(R("fav", NS * x, NS * x + NS), R("gs", 64 * x, 64 * x + 8)))

    states(0, 0, 24)
    for b in range(4):
        block(0, b, b, 0)
        block(0, b, b, 1)
        if b == 1:
            ts(R("wb"), R("lane", 0, 144), COL(C15), ALU.is_equal)
            for x in range(2):
                ts(R("av", 8 * x + 4, 8 * x + 5), COL(RCOL), 0.0, ALU.is_equal, -15.5, ALU.mult)
    first_lists(0)
    layout(0)
    first_sources(0, 0)
    ts(MAT(SEL, name="matf"), GI, COL(GCOL), ALU.is_equal, COL(SG), ALU.mult)
    cp(R("tu", 0, N), PS(6, 0, N))
    for i, val in ((BN, -1.0), (BKS, 1.0 / (ZS * 2048)), (NKS, -1.0 / (ZS * 2048))):
        act(MAT(i), MAT(BP), scale=val)

    def constants(step):
        if step == 0:
            fill(R("step"), TAG)
            thresholds(0, 0)
            count(0, None, 1)
            fill(R("step", step=8), 2.0 ** 26)
            thresholds(0, 1)
            ts(ROW(RR), R("jm", 0, 128, parts=1), -1.0 / 2048, ALU.mult, -15.0 / 4096, ALU.add)
        if step == 2:
            act(MAT(BB), MAT(BP), scale=4096.0)
        if step == 1:
            ts(COL(TF + 2, 8), R("tm", 8, 9, parts=8), 0.5 - 16 * XH, ALU.add)
            ts(MAT(BK5, name="matf"), GI4, COL(G4), ALU.is_equal, 0.5, ALU.mult)
            ts(COL(HI, 8), COL(TF + 2, 8), M7, ALU.add, M7, ALU.subtract)
            for h in range(2):
                ts(MAT(BES + h), GI4, COL(P4 + 1 if h else GCOL), ALU.is_equal, 1.0 / 2048, ALU.mult)
            tt(COL(LO, 8), COL(TF + 2, 8), COL(HI, 8), ALU.subtract)
            ts(R("nm"), R("jm"), COL(RCOL), ALU.not_equal, -2.0 ** 44, ALU.mult)
            for x in range(2):
                ts(MAT(MGH + x, 8), R("gi", 128, 256, parts=8), COL(P4 if x else PCOL, 8), ALU.is_equal, COL(HI, 8), ALU.mult)
                ts(MAT(MGL + x, 8), R("gi", 128, 256, parts=8), COL(P4 if x else PCOL, 8), ALU.is_equal, COL(LO, 8), ALU.mult)

    def tables(x):
        states(x, 32, 56)
        cp(R("gq", 64 * x, 64 * x + 32), R("gp", 64 * x, 64 * x + 32))
        cp(R("L", x * NS, x * NS + NS), R("fav", x * NS, x * NS + NS))

    ready = {"tables": tables, "constants": constants, "keys": first_keys, "block": lambda b, bank, step: block(1, b, bank, step),
             "states": states, "lists": first_lists, "layout": layout, "origins": first_sources, "thresholds": thresholds,
             "tile": lambda: cp(R("tu", N, K), PS(6, 0, N))}

    def steps(n):
        x, t = n % 2, n // 2
        c = t % C
        o, s = c * K, x * N
        m, r = (2 * x + c) * N, (2 * x + 1 - c) * N
        d = 1 + t % (NR - 1)
        last, final = t == RO - 1, t >= RO - C
        Ww, Lw = R("W", x * WN, x * WN + WN), R("L", x * NS, x * NS + NS)
        Z, Z2, Z3, HS, AS = PS(4, 0, N), PS(5, 0, N), PS(5, N, K), PS(0, 0, N), PS(1, 0, 2)
        CST, X2 = R("cst"), PS(5, K, K + N)
        rows = slice(HP * x, HP * x + HP)

        def S(name, a=0, b=N, w=1, step=1):
            return R(name, w * (s + a), w * (s + b), step)

        def M(name):
            return R(name, m, m + N)

        def told(k=n):
            return R("x3", k * N, k * N + N)

        def out(eng, dst, col, name, at, ext=None):
            for h in range(2):
                store(eng, dst[rows, col + h * N:col + h * N + N], RH(name, h, at, at + N), ext=ext)

        parts = [(ND, N, 0, 8), (ND, N, 8, 16)] if n else [(0, 64, 0, 16), (64, N, 0, 16)]

        def old(a, b):
            return R("bo", m + a, m + b) if t < C else R("x3", (n - 2 * C) * N + a, (n - 2 * C) * N + b)

        def far(j):
            a, b = parts[j][:2]
            act(S("far", a, b, 16), IX(Ww, R("s16", m + a, m + b)), scale=1.0 / U, bias=128.0 - (WT + 1024.0) / U)

        def far_v():
            tt(S("far", 0, ND, 16), IX(Ww, R("s16", m, m + ND)), REP(m), ALU.subtract)

        def place(j, p):
            a, b, p0, p1 = parts[j]
            return 1024 * j + 512 + (p - (p0 + p1) // 2) * (b - a), 16 * (s + a) + p * (b - a)

        def sub(j):
            a, b, p0, p1 = parts[j]
            for p in range(p0, p1):
                at = place(j, p)[0]
                mm(R("ps", at, at + b - a), [(MAT(NI), old(a, b)), (MAT(ID), R("far", 16 * (s + a) + p, 16 * (s + b), 16))])

        def absolute(j):
            (q0, a0), (q1, a1) = place(j, parts[j][2]), place(j, parts[j][3])
            act(R("ad", a0, a1), R("ps", q0, q1), func=ACT.Abs, scale=ZS)

        def abs_v():
            act(S("ad", 0, ND, 16), S("far", 0, ND, 16), func=ACT.Abs, scale=ZS / U)

        def red_v():
            mm(PS(4, 0, ND), [(R("wb", 15 - p, 143 - p), R("ad", 16 * s + p, 16 * (s + ND), 16)) for p in range(16)], first=False)

        def seed():
            act(R("seed", m, m + ND), old(0, ND), scale=U, bias=X0 + WT + 1024.0)

        def repeat():
            for p in range(16):
                to, of = REP(m, p), R("seed", m, m + ND)
                add("g", lambda q, to=to, of=of: q.affine_select(to[0], of[0], [[0, ND]], ALU.is_ge, 0.0, 0, 0), [to], [of])

        def limits():
            pairs = [(ROW(C0 if t < C else C2), R("cst", parts=1)), (MAT(DT + x, name="math"), CST), (MAT(EV + (x if t else 0), name="math"), CST)]
            if t >= C:
                pairs += [(MAT(BB), M("sg"))]
            mm(Z, pairs, last=False)

        def red(j):
            a, b, p0, p1 = parts[j]
            mm(PS(4, a, b), [(R("wb", 15 - p, 143 - p), R("ad", place(j, p)[1], place(j, p + 1)[1])) for p in range(p0, p1)],
               first=False, last=j == 1 and n == 0)

        def low(a, b):
            ts(S("ya", a, b, 8), IX(Ww, R("tu", s + a // 2, s + b // 2)), -8 * TAG, ALU.add)

        def low_a(a, b):
            act(S("ya", a, b, 8), IX(Ww, R("tu", s + a // 2, s + b // 2)), bias=-8 * TAG)

        def high(a, b):
            tt(S("yb", a, b, 8), IX(Ww, R("tu", s + 64 + a // 2, s + 64 + b // 2)), S("ya", a, b, 8), ALU.min)

        def scan(a=0, b=N):
            so, d0, d1 = S("sc", a, b, 8), R("step", 0, 8 * (b - a)), S("yb", a, b, 8)
            add("v", lambda q: q.tensor_tensor_scan(so[0], d0[0], d1[0], 0.0, ALU.add, ALU.min), [so], [d0, d1])

        def known():
            pairs = [(MAT(MGH + x, 8), R("cst", parts=8)), (MAT(MGL + x, 8), R("cst", parts=8))]
            if t == 0:
                pairs += [(MAT(BP), M("bo"))]
            else:
                pairs += [(MAT(BN if c else BP), S("gap")), (MAT(BP), told(n - 2))]
            return pairs

        def cuts():
            mm(Z2, known(), last=False)

        def lapsed():
            tt(Z, Z, M("ko"), ALU.max)

        def based():
            tt(Z, Z, M("kb"), ALU.min)

        def least():
            tt(S("k2"), Z, R("sc", 8 * s + 7, 8 * (s + N), 8), ALU.min)

        def number():
            ts(S("x2h"), S("k2"), 1.0 / U, ALU.mult, XH + 128 - 0.140625, ALU.add)
            mm(Z2, [(MAT(BN), S("x2h"))], first=False)
            mm(X2, [(ROW(CH), ONE), (MAT(ID), S("x2h"))])

        def denied():
            tt(S("back"), Z2, M("bo"), ALU.min)

        def tell():
            tt(told(), X2, S("back"), ALU.max)
            send(n)
            if final:
                out("s", T.yx, o, "x3", n * N)

        def reset(step):
            if final and step == 0:
                tt(Z, Z2, M("kb"), ALU.min)
            if final and step == 1:
                tt(S("k2"), Z, S("k2"), ALU.max)

        def row():
            mm(Z3, [(MAT(ID), R("nm", t, t + N)), (MAT(BN), S("x2h")), (MAT(BP), told())])

        def first():
            ts(S("h0"), R("ya", 8 * s + 7, 8 * (s + N), 8), 1.0 / U, ALU.mult, XH + 128, ALU.add)

        def entry():
            mm(HS, [(ROW(RR), ONE), (MAT(BKS), S("h0")), (ROW(PM0), ONE), (ROW(NM0), ONE), (MAT(NKS), S("h0"))])

        def pick():
            act(S("pick"), HS, func=ACT.Relu, scale=65536.0 * 128, bias=COL(PB))

        def chosen():
            at = 64 * x + 32 + 16 * c
            tt(S("sel"), IX(Lw, R("gs", at, at + 8)), S("pick"), ALU.min)

        def put():
            act(M("sg"), Z3, func=ACT.Sign, bias=(16 * XH - 0.5) * ZS, acc=None if last else R("av", 8 * x, 8 * x + 1))

        def merge():
            for h in range(2):
                mm(PS(6, K + h * N, K + h * N + N), [(MAT(SE + h), S("t16")), (MAT(NE + h), M("sg"))])
                mm(PS(6, h * N, h * N + N), [(MAT(BES + h), S("sel")), (MAT(DE + h), M("sg"))])

        def counted():
            if not last:
                mm(AS, [(MAT(BK5, name="matf"), R("av", 8 * x, 8 * x + 2)), (MAT(SEL, name="matf"), R("av", 8 * x + 4, 8 * x + 6))])

        def ab():
            act(R("ab"), PS(6, 0, V), func=ACT.Relu, scale=2048.0, bias=-2048.0)

        def edit():
            at = 64 * x + 16 * c
            tt(IX(Lw, R("gq", at, at + 16)), R("ab", 0, K), R("ab", K, V), ALU.add)
            if last:
                store("a", T.yl[rows, :], RH("L", 0, x * NS, x * NS + NS))

        def window(step, name, col, bank, ext=None):
            if last:
                return
            if step == 0:
                columns(PS(bank, 0, K), K)
                for h in range(2):
                    mm(PS(bank, h * N, h * N + N), [(MAT(UE + h), R(name, n * N, n * N + N))], first=False, last=h == 1, ext=ext)
            else:
                act(R("W", x * WN + col, x * WN + col + K), PS(bank, 0, K), bias=WT + col)

        def own(step):
            window(step, "x3", o, 7)

        def copies(step):
            window(step, "land", d * V + o, 2, arrived(n))

        def keep():
            out("s", T.yx, d * V + o, "land", n * N, arrived(n))

        def source():
            ts(S("si"), S("k2"), 2047, ALU.bitwise_and)

        def sources():
            cp(M("sf" if final else "s16"), S("si"))
            if final:
                out("s", T.ys, o, "sf", m)

        def aged():
            if not final:
                ts(M("ko"), S("k2"), ~(63 << 11), ALU.bitwise_and)

        def tally(step):
            if not last:
                count(x, PS(1, 0, 1), step)

        def other(step):
            if t == 0:
                first_keys(x, 1, 7, step)
                if step == 0:
                    first_sources(x, 1)
                if step == 2:
                    tt(S("gap"), M("bo"), R("bo", r, r + N), ALU.subtract)

        def grantors():
            if not last:
                at = 64 * x + 16 - 16 * c
                cp(S("t16"), IX(Lw, R("gs", at, at + 8)))

        def lay():
            if not last:
                layout(x)

        def offsets():
            if not last:
                cp(S("tu"), PS(6, 0, N))

        return {"far_v": far_v, "abs_v": abs_v, "red_v": red_v, "seed": seed, "repeat": repeat,
                "far": far, "sub": sub, "abs": absolute, "limits": limits, "red": red, "low": low, "low_a": low_a, "high": high,
                "scan": scan, "cuts": cuts, "lapsed": lapsed, "based": based, "least": least, "number": number, "counted": counted,
                "denied": denied, "tell": tell, "reset": reset, "row": row, "first": first, "entry": entry, "pick": pick,
                "chosen": chosen, "put": put, "merge": merge, "ab": ab, "edit": edit, "own": own, "copies": copies,
                "keep": keep, "source": source, "sources": sources, "aged": aged, "tally": tally, "other": other,
                "grantors": grantors, "lay": lay, "offsets": offsets}

    order = [s.split() for s in ORDER.split(",")]
    turns = {n: steps(n) for n in range(2 * RO)}
    for name, *args in [s.split() for s in OPENING.split(",")]:
        dict(turns[name.count(">")], **ready)[name.lstrip(">")](*[int(a) for a in args])
    closing = [[s.split() for s in c.split(",")] for c in CLOSING]
    for n in range(1, 2 * RO + 1):
        for name, *args in (closing[n - 2 * RO + 1] if n >= 2 * RO - 1 else order):
            table = turns.get(n - name.count("<") + name.count(">"), {})
            if name.lstrip("<>") in table:
                table[name.lstrip("<>")](*[int(a) for a in args])

    emit(ops, queue, T, 2 * RO * neng)


def emit(ops, queue, T, nsent):
    def meet(xs, ys):
        return any(x[0] == y[0] and x[1] < y[2] and y[1] < x[2] and x[3] < y[4] and y[3] < x[4] for x in xs for y in ys)

    def banks(x):
        s = set()
        for r in x["rd"] + x["wr"]:
            if r[0] == "ps":
                s |= set(range(r[1] // 512, (r[2] - 1) // 512 + 1))
        return s

    known = {e: {} for e in ENGINES}
    clock, waits, signal = [], [], set()
    bk = [banks(x) for x in ops]
    for j, x in enumerate(ops):
        e, need = x["e"], {}
        for i in range(j - 1, -1, -1):
            y = ops[i]
            if y["e"] == "p" and ("p" in need or e == "p" or known[e].get("p", -1) >= i):
                continue
            if y["dma"] == "remote":
                continue
            key = ("dma", i) if y["dma"] else y["e"]
            if key in need or known[e].get(key, -1) >= i or (key == "p" and e == "p"):
                continue
            if meet(x["rd"], y["wr"]) or meet(x["wr"], y["wr"]) or meet(x["wr"], y["rd"]) or (y["e"] != e and bk[i] & bk[j]):
                need[key] = i
        w = []
        for key, i in sorted(need.items(), key=lambda kv: -kv[1]):
            if known[e].get(key, -1) >= i:
                continue
            w.append(i)
            signal.add(i)
            for k2, i2 in clock[i].items():
                known[e][k2] = max(known[e].get(k2, -1), i2)
        waits.append(w)
        ck = dict(known[e])
        ck[("dma", j) if x["dma"] else e] = j
        clock.append(ck)
    count = {e: 0 for e in ENGINES}
    mark, ndma, open_dma = {}, 0, {}
    for j, x in enumerate(ops):
        e, q = x["e"], queue[x["e"]]
        for i in waits[j]:
            sem, n = mark[i]
            q.wait_ge(sem, n)
            open_dma.pop(i, None)
        for sem, n in x["ext"] or []:
            q.wait_ge(sem, n)
        ins = x["fn"](q)
        if x["dma"] == "remote":
            continue
        if x["dma"]:
            mark[j] = (T.sem["d%d" % ndma], 16)
            ndma += 1
            ins.then_inc(mark[j][0], 16)
            open_dma[j] = e
        elif j in signal:
            count[e] += 1
            mark[j] = (T.sem["e_" + e], count[e])
            ins.then_inc(mark[j][0], 1)
    for j, e in open_dma.items():
        queue[e].wait_ge(*mark[j])
    queue["g"].wait_ge(T.sem.sent, nsent)
